import numpy as np
import ml_dtypes


def mxq(x, axis, fmt="e4m3"):
    dtype, down = {"e4m3": (ml_dtypes.float8_e4m3fn, 7), "e5m2": (ml_dtypes.float8_e5m2, 14)}[fmt]
    v = np.moveaxis(np.asarray(x, np.float32).astype(ml_dtypes.bfloat16).astype(np.float64), axis, -1)
    blocks = v.reshape(v.shape[:-1] + (-1, 32))
    amax = np.abs(blocks).max(-1, keepdims=True)
    byte = np.maximum(np.where(amax > 0, np.frexp(amax)[1] - 1 + 127, 0) - down, 1)
    scale = np.exp2(byte - 127.0)
    codes = (blocks / scale).astype(np.float32).astype(dtype).astype(np.float64)
    return np.moveaxis((codes * scale).reshape(v.shape), -1, axis)


WIDE = False


def mx_kscale(k):
    if not WIDE:
        return np.ones(k)
    levels = np.array([10, -10, 5, -5, 0])
    if k % 512:
        return np.exp2(np.random.permutation(np.resize(levels, k // 32))).repeat(32)
    a = np.empty((k // 512, 16))
    for p in range(k // 512):
        a[p, :8] = np.random.permutation(np.resize(levels, 8))
        for g in range(8):
            far = levels[np.abs(levels - a[p, g]) >= 10]
            a[p, g + 8] = far[np.random.randint(len(far))]
    return np.exp2(a.ravel()).repeat(32)


BF16 = ml_dtypes.bfloat16


def bf(x):
    return np.asarray(x, np.float32).astype(BF16)


def f64(x):
    return np.asarray(x).astype(np.float64)


E2M1 = np.array([0.0, 0.5, 1.0, 1.5, 2.0, 3.0, 4.0, 6.0, -0.0, -0.5, -1.0, -1.5, -2.0, -3.0, -4.0, -6.0])


def pack_weight(w, fmt):
    k, n = w.shape
    w = f64(bf(w)).reshape(k // 32, 32, n)
    amax = np.abs(w).max(1)
    if fmt == "e4m3":
        byte = np.frexp(amax)[1] - 1 + 127 - 7
    else:
        mant, ex = np.frexp(amax / 6.0)
        byte = np.where(mant > 0.5, ex, ex - 1) + 127
    byte = np.clip(np.where(amax > 0, byte, 1), 1, 254)
    scaled = (w * np.exp2(127.0 - byte)[:, None, :]).reshape(k, n).astype(np.float32)
    by_word = np.ascontiguousarray(scaled.reshape(k // 512, 128, 4, n).transpose(0, 1, 3, 2))
    if fmt == "e4m3":
        words = by_word.astype(ml_dtypes.float8_e4m3fn).view(np.uint8)
    else:
        c = by_word.astype(ml_dtypes.float4_e2m1fn).view(np.uint8) & 0xF
        words = c[..., 0::2] | (c[..., 1::2] << 4)
    return np.ascontiguousarray(words), np.ascontiguousarray(byte.astype(np.uint8).reshape(k // 512, 16, n))


def unpack_weight(words, scales, fmt):
    g, p, n, _ = words.shape
    if fmt == "e4m3":
        vals = np.ascontiguousarray(words).view(ml_dtypes.float8_e4m3fn).astype(np.float64)
    else:
        nib = np.empty((g, p, n, 4), np.uint8)
        nib[..., 0::2] = words & 0xF
        nib[..., 1::2] = words >> 4
        vals = E2M1[nib]
    vals = vals * np.repeat(np.exp2(scales.astype(np.float64) - 127.0), 8, axis=1)[..., None]
    return vals.transpose(0, 1, 3, 2).reshape(g * 512, n)
def pack4(w):
    words, scales = pack_weight(w, "e2m1")
    return words.reshape(words.shape[0], 128, -1), scales


def unpack4(words, scales):
    return unpack_weight(words.reshape(words.shape[0], 128, -1, 2), scales, "e2m1")


M, T, K, R, F, D = 1024, 1536, 1024, 512, 1024, 1024

SIGMA = 0.7
EPS = 1e-6


def draw0():
    s, t, u = mx_kscale(K), mx_kscale(F), mx_kscale(T)
    length = np.exp(0.15 * np.random.standard_normal(T))
    omega_words, omega_scales = pack4(SIGMA * np.random.standard_normal((K, R)) / np.sqrt(K) / s[:, None])
    state_words, state_scales = pack_weight(np.random.standard_normal((F, D)) / t[:, None], "e4m3")
    return {"queries": bf(np.random.standard_normal((M, K)) * s),
            "keys": bf(np.random.standard_normal((T, K)) * length[:, None] * s),
            "values": bf(np.random.standard_normal((T, D)) / u[:, None]),
            "omega_words": omega_words, "omega_scales": omega_scales,
            "state_words": state_words, "state_scales": state_scales,
            "half_norm": bf(0.5 * SIGMA ** 2 * length ** 2),
            "read": bf((1 + 0.1 * np.random.standard_normal(F)) / np.sqrt(F) * t),
            "write": bf((1 + 0.1 * np.random.standard_normal(T)) / np.sqrt(T) * u),
            "keep": bf((0.9 + 0.05 * np.random.standard_normal(F)) * t),
            "gain": bf(1 + 0.1 * np.random.standard_normal(D))}


def core(queries, keys, values, omega_words, omega_scales, state_words, state_scales, half_norm, read, write, keep, gain):
    omega = unpack4(omega_words, omega_scales)
    state = unpack_weight(state_words, state_scales, "e4m3")
    a = mxq(f64(queries), 1, "e4m3") @ omega
    b = mxq(f64(keys), 1, "e4m3") @ omega
    fq = np.concatenate([np.exp(a), np.exp(-a)], axis=1) * f64(read)
    h = f64(half_norm)[:, None]
    fk = np.concatenate([np.exp(b - h), np.exp(-b - h)], axis=1) * f64(write)[:, None]
    c = mxq(fq, 1, "e4m3") @ state
    y = c / np.sqrt(np.mean(c * c, axis=1, keepdims=True) + EPS) * f64(gain)
    d = mxq(fk, 0, "e4m3").T @ mxq(f64(values), 0, "e4m3")
    new_state = f64(keep)[:, None] * state + d
    return y, new_state


def e4m3fn_bytes(y):
    return np.clip(np.asarray(y, np.float64), -448.0, 448.0).astype(np.float32).astype(ml_dtypes.float8_e4m3fn).view(np.uint8)


def e4m3fn_values(b):
    return np.asarray(b, np.uint8).view(ml_dtypes.float8_e4m3fn).astype(np.float64)


def setup_inputs():
    d = draw0()
    x0 = np.asarray(d['values']).astype(np.float64)
    s = (np.max(np.abs(x0), axis=(1,), keepdims=True) / 448.0).astype(np.float32)
    out = {}
    for k, v in d.items():
        if k == 'values':
            out['values_bytes'] = e4m3fn_bytes(x0 / s.astype(np.float64))
            out['values_scale'] = s
        else:
            out[k] = v
    return out


def reference(queries, keys, values_bytes, values_scale, omega_words, omega_scales, state_words, state_scales, half_norm, read, write, keep, gain):
    return core(queries, keys, e4m3fn_values(values_bytes) * values_scale.astype(np.float64), omega_words, omega_scales, state_words, state_scales, half_norm, read, write, keep, gain)

@@ -1,0 +1,742 @@
+from contextlib import ExitStack
+
+import concourse.mybir as mybir
+from concourse.masks import make_identity
+
+F32 = mybir.dt.float32
+BF16 = mybir.dt.bfloat16
+I32 = mybir.dt.int32
+U32 = mybir.dt.uint32
+U8 = mybir.dt.uint8
+FP8 = mybir.dt.float8_e4m3fn
+FP8X4 = mybir.dt.float8_e4m3fn_x4
+FP4X4 = mybir.dt.float4_e2m1fn_x4
+ACTF = mybir.ActivationFunctionType
+ALU = mybir.AluOpType
+
+P = 128
+M, T, K, R, F, D = 1024, 1536, 1024, 512, 1024, 1024
+EPS = 1e-6
+FLOPS = 2 * (M * K * R + T * K * R + M * F * D + T * F * D)
+
+TPB, ABB, CB, SDB, KSB = 1,2,2,3,4
+KG = K // 512
+TG = T // 512
+FG = F // 512
+WIDEN_ON_VECTOR = (0, 1, 2, 3, 7, 11)
+
+
+def tile_performer_state_step_f7_kernel(
+    tc, queries, keys, values_bytes, values_scale, omega_words, omega_scales,
+    state_words, state_scales, half_norm, read, write, keep, gain, out_0, out_1,
+):
+    nc = tc.nc
+    with ExitStack() as ctx:
+        cst = ctx.enter_context(tc.tile_pool(name="cst", bufs=1))
+        raw = ctx.enter_context(tc.tile_pool(name="raw", bufs=1))
+        wk = ctx.enter_context(tc.tile_pool(name="wk", bufs=3))
+        ps = ctx.enter_context(tc.psum_pool(name="ps", bufs=2))
+        ctx.enter_context(tc.manual_schedule())
+
+        kview = keys.rearrange("(g p t) k -> g t p k", p=P, t=4)
+        kraw = []
+        for i in range(12):
+            kr = raw.tile([P, K], BF16, name=f"kraw{i}", align_bytes=64)
+            kraw.append(kr)
+        qraw = []
+        for m in range(8):
+            qr = raw.tile([P, K], BF16, name=f"qraw{m}", align_bytes=64)
+            qraw.append(qr)
+        vbytes = []
+        for g in range(TG):
+            vb = raw.tile([P, 4, D], U8, name=f"vbytes{g}", align_bytes=64)
+            vbytes.append(vb)
+
+        ow = cst.tile([P, KG, 2 * R], U8, name="ow", align_bytes=64)
+        osc = cst.tile([P, KG, R], U8, name="osc", align_bytes=64)
+        sw = cst.tile([P, FG, 4 * D], U8, name="sw", align_bytes=64)
+        ssc = cst.tile([P, FG, D], U8, name="ssc", align_bytes=64)
+        wr = cst.tile([P, TG, 4], BF16, name="wr")
+        hn = cst.tile([P, TG, 4], BF16, name="hn")
+        vs = cst.tile([P, TG, 4], F32, name="vs")
+        rd = cst.tile([P, FG, 4], BF16, name="rd")
+        kz = cst.tile([P, P], BF16, name="kz")
+        gn = cst.tile([P, D], BF16, name="gn")
+
+        nc.gpsimd.memset(osc[:].bitcast(I32), 0)
+        identf = cst.tile([P, P], F32, name="identf")
+        make_identity(nc, identf[:])
+        nc.gpsimd.memset(kz[:], 0.0)
+        nc.gpsimd.memset(ssc[:].bitcast(I32), 0)
+
+        vview = values_bytes.rearrange("(g p t) d -> g p t d", p=P, t=4)
+        oview = omega_scales.rearrange("g (q r) n -> r q g n", r=4)
+        sview = state_scales.rearrange("g (q r) n -> r q g n", r=4)
+        nc.scalar.dma_start(out=wr[:], in_=write.rearrange("(g p t) -> p g t", p=P, t=4))
+        nc.scalar.dma_start(out=vs[:], in_=values_scale.rearrange("(g p t) o -> p g (t o)", p=P, t=4))
+        nc.scalar.dma_start(out=hn[:], in_=half_norm.rearrange("(g p t) -> p g t", p=P, t=4))
+        nc.sync.dma_start(out=kraw[0][:], in_=kview[0, 0])
+        nc.sync.dma_start(out=kraw[1][:], in_=kview[0, 1])
+        nc.sync.dma_start(out=vbytes[0][:], in_=vview[0])
+        nc.sync.dma_start(out=ow[:], in_=omega_words.rearrange("g p b -> p g b"))
+        for r in range(4):
+            nc.sync.dma_start(out=osc[r:P:32, :, :].bitcast(I32), in_=oview[r].bitcast(I32))
+        nc.sync.dma_start(out=kraw[2][:], in_=kview[0, 2])
+        nc.sync.dma_start(out=kraw[3][:], in_=kview[0, 3])
+        nc.sync.dma_start(out=vbytes[1][:], in_=vview[1])
+        for t in range(4):
+            nc.sync.dma_start(out=kraw[4 + t][:], in_=kview[1, t])
+        nc.sync.dma_start(out=rd[:], in_=read.rearrange("(g p t) -> p g t", p=P, t=4))
+        nc.sync.dma_start(out=kz[0:8, :], in_=keep.rearrange("(c p) -> c p", p=P))
+        nc.sync.dma_start(out=vbytes[2][:], in_=vview[2])
+        for t in range(4):
+            nc.sync.dma_start(out=kraw[8 + t][:], in_=kview[2, t])
+        nc.sync.dma_start(out=sw[:], in_=state_words.rearrange("g p n t -> p g (n t)"))
+        for r in range(4):
+            nc.sync.dma_start(out=ssc[r:P:32, :, :].bitcast(I32), in_=sview[r].bitcast(I32))
+        for m in range(8):
+            nc.sync.dma_start(out=qraw[m][:], in_=queries[P * m : P * (m + 1), :])
+        nc.sync.dma_start(out=gn[:], in_=gain.partition_broadcast(P))
+
+        quarter = cst.tile([P, TG * 4], F32, name="quarter")
+        nc.vector.memset(quarter[:], 0.25)
+        mhalf = cst.tile([P, 1], F32, name="mhalf")
+        nc.vector.memset(mhalf[:], -0.5)
+        kbias = cst.tile([P, TG * 4], F32, name="kbias")
+        vss = cst.tile([P, TG * 4], F32, name="vss")
+
+        sel = cst.tile([P, 512, 4], BF16, name="sel", align_bytes=64)
+        nc.gpsimd.memset(sel[:].rearrange("p f t -> p (f t)"), 0.0)
+        nc.gpsimd.affine_select(
+            out=sel[:], in_=sel[:], compare_op=ALU.not_equal, fill=1.0, base=0,
+            pattern=[[1, 512], [-1, 4]], channel_multiplier=-4,
+        )
+        selq = cst.tile([P, 512], U32, name="selq", align_bytes=64)
+        sels = cst.tile([P, 512], U8, name="sels", align_bytes=64)
+
+        owp = cst.tile([P, KG, 4, P, 2], U8, name="owp", align_bytes=64)
+        osp = cst.tile([P, KG, 4, P], U8, name="osp", align_bytes=64)
+        keepn = cst.tile([P, 8], F32, name="keepn")
+        pkq, pks, vq, vsc = [], [], [], []
+        for g in range(TG):
+            a = cst.tile([P, F], U32, name=f"pkq{g}", align_bytes=64)
+            b = cst.tile([P, F], U8, name=f"pks{g}", align_bytes=64)
+            c = cst.tile([P, D], U32, name=f"vq{g}", align_bytes=64)
+            d = cst.tile([P, D], U8, name=f"vsc{g}", align_bytes=64)
+            pkq.append(a)
+            pks.append(b)
+            vq.append(c)
+            vsc.append(d)
+        st = {}
+
+        def rows(i):
+            return kraw[i] if i < 12 else qraw[i - 12]
+
+        def transposes(i):
+            words = rows(i)[:].bitcast(F32)
+            tp = ps.tile([P, KG, 2, P], F32, name="tp", bufs=TPB)
+            for g in range(KG):
+                for u in range(2):
+                    nc.tensor.transpose(
+                        tp[:, g, u, :], words[:, 256 * g + u : 256 * (g + 1) : 2], identf[:]
+                    )
+            st["tp", i] = tp
+
+        def copy_out(i):
+            xt = wk.tile([P, KG * P * 4], BF16, name="xt", align_bytes=64)
+            nc.scalar.copy(
+                out=xt[:].bitcast(F32).rearrange("p (g r u) -> p g r u", g=KG, u=2),
+                in_=st["tp", i][:].rearrange("p g u r -> p g r u"),
+            )
+            st["xt", i] = xt
+
+        def quantize_rows(i):
+            xq = wk.tile([P, KG * P], U32, name="xq", align_bytes=64)
+            xs = wk.tile([P, KG * P], U8, name="xs", align_bytes=64)
+            nc.vector.quantize_mx(out=xq[:].bitcast(FP8X4), scales=xs[:], in_=st["xt", i][:])
+            st["xq", i] = (xq, xs)
+
+        def widen(i):
+            g, t = divmod(i, 4)
+            if ("vpl", g) not in st:
+                vpl = wk.tile([P, 4, D], BF16, name="vpl", bufs=2, align_bytes=64)
+                st["vpl", g] = vpl
+            dst = st["vpl", g][:, t, :]
+            src = vbytes[g][:, t, :].bitcast(FP8)
+            if i in WIDEN_ON_VECTOR:
+                nc.vector.tensor_scalar(
+                    out=dst, in0=src, scalar1=vss[:, i : i + 1], scalar2=None, op0=ALU.mult
+                )
+            else:
+                nc.scalar.activation(out=dst, in_=src, func=ACTF.Copy, scale=vss[:, i : i + 1])
+
+        def interleave(dst, planes):
+            nc.vector.tensor_copy(
+                out=dst.rearrange("p (c i t) -> p c t i", i=4, t=4),
+                in_=planes.rearrange("p t (c i) -> p c t i", i=4),
+            )
+
+        def values_interleave(g, h):
+            if ("vint", g) not in st:
+                vint = wk.tile([P, D * 4], BF16, name="vint", bufs=2, align_bytes=64)
+                st["vint", g] = vint
+            half = slice(512 * h, 512 * (h + 1))
+            interleave(st["vint", g][:, 2048 * h : 2048 * (h + 1)], st["vpl", g][:, :, half])
+
+        def values_quantize(g):
+            nc.vector.quantize_mx(
+                out=vq[g][:].bitcast(FP8X4), scales=vsc[g][:], in_=st["vint", g][:]
+            )
+
+        def key_product(i):
+            kq, ks = st["xq", i]
+            bank = ps.tile([P, R], F32, name="ab", bufs=ABB)
+            for c in range(KG):
+                nc.tensor.matmul_mx(
+                    out=bank[:],
+                    lhsT=kq[:, P * c : P * (c + 1)].bitcast(FP8X4),
+                    lhsT_scale=ks[:, P * c : P * (c + 1)],
+                    rhs=ow[:, c, :].bitcast(FP4X4),
+                    rhs_scale=osc[:, c, :],
+                    start=(c == 0),
+                    stop=(c == KG - 1),
+                )
+            st["b", i] = bank
+
+        def key_exp(i, s):
+            g, t = divmod(i, 4)
+            if ("pl", g) not in st:
+                pl = wk.tile([P, 2, 4, R], BF16, name="pl", bufs=2, align_bytes=64)
+                st["pl", g] = pl
+            nc.scalar.activation(
+                out=st["pl", g][:, s, t, :], in_=st["b", i][:], func=ACTF.Exp,
+                bias=kbias[:, i : i + 1], scale=1.0 - 2.0 * s,
+            )
+
+        def features_interleave(g, s):
+            pint = wk.tile([P, R * 4], BF16, name="pint", align_bytes=64)
+            interleave(pint[:], st["pl", g][:, s])
+            st["pint", g, s] = pint
+
+        def features_quantize(g, s):
+            nc.vector.quantize_mx(
+                out=pkq[g][:, R * s : R * (s + 1)].bitcast(FP8X4),
+                scales=pks[g][:, R * s : R * (s + 1)],
+                in_=st["pint", g, s][:],
+            )
+
+        def permute_omega(c):
+            nc.vector.tensor_copy(
+                out=owp[:, c], in_=ow[:, c].rearrange("p (m t b) -> p t m b", t=4, b=2)
+            )
+
+        def permute_scales(c):
+            nc.vector.tensor_copy(
+                out=osp[:, c], in_=osc[:, c].rearrange("p (m t) -> p t m", t=4)
+            )
+
+        def keep_columns():
+            kzf = cst.tile([P, P], F32, name="kzf")
+            nc.vector.tensor_copy(out=kzf[:], in_=kz[:])
+            st["kzf"] = kzf
+
+        def keep_turn():
+            kt = ps.tile([P, P], F32, name="ab", bufs=ABB)
+            nc.tensor.transpose(kt[:], st["kzf"][:], identf[:])
+            st["kt"] = kt
+
+        def keep_copy():
+            kt = st["kt"]
+            nc.vector.tensor_copy(out=keepn[:], in_=kt[:, 0:8])
+
+        def query_product(m):
+            qq, qs = st["xq", 12 + m]
+            bank = ps.tile([P, 4, P], F32, name="ab", bufs=ABB)
+            for t in range(4):
+                for c in range(KG):
+                    nc.tensor.matmul_mx(
+                        out=bank[:, t, :],
+                        lhsT=owp[:, c, t].rearrange("p m b -> p (m b)").bitcast(FP4X4),
+                        lhsT_scale=osp[:, c, t, :],
+                        rhs=qq[:, P * c : P * (c + 1)].bitcast(FP8X4),
+                        rhs_scale=qs[:, P * c : P * (c + 1)],
+                        start=(c == 0),
+                        stop=(c == KG - 1),
+                    )
+            st["a", m] = bank
+
+        def query_exp(m, s):
+            if ("ex", m) not in st:
+                ex = wk.tile([P, 2, P, 4], F32, name="ex", bufs=2)
+                st["ex", m] = ex
+            nc.scalar.activation(
+                out=st["ex", m][:, s], in_=st["a", m][:].rearrange("p t n -> p n t"), func=ACTF.Exp,
+                scale=1.0 - 2.0 * s,
+            )
+
+        def query_scale(m):
+            pq = wk.tile([P, 2, P, 4], BF16, name="pq", bufs=2, align_bytes=64)
+            nc.vector.tensor_tensor(
+                out=pq[:], in0=st["ex", m][:],
+                in1=rd[:].unsqueeze(2).to_broadcast([P, 2, P, 4]), op=ALU.mult,
+            )
+            st["pq", m] = pq
+
+        def query_quantize(m):
+            pqq = wk.tile([P, 2 * P], U32, name="pqq", bufs=2, align_bytes=64)
+            pqs = wk.tile([P, 2 * P], U8, name="pqs", bufs=2, align_bytes=64)
+            nc.vector.quantize_mx(
+                out=pqq[:].bitcast(FP8X4), scales=pqs[:],
+                in_=st["pq", m][:].rearrange("p s n t -> p (s n t)"),
+            )
+            st["pqq", m] = (pqq, pqs)
+
+        def read_product(m, h):
+            pqq, pqs = st["pqq", m]
+            cb = ps.tile([P, 512], F32, name="cb", bufs=CB)
+            for s in range(2):
+                nc.tensor.matmul_mx(
+                    out=cb[:],
+                    lhsT=pqq[:, P * s : P * (s + 1)].bitcast(FP8X4),
+                    lhsT_scale=pqs[:, P * s : P * (s + 1)],
+                    rhs=sw[:, s, 2048 * h : 2048 * (h + 1)].bitcast(FP8X4),
+                    rhs_scale=ssc[:, s, 512 * h : 512 * (h + 1)],
+                    start=(s == 0),
+                    stop=(s == 1),
+                )
+            st["c", m, h] = cb
+
+        def read_square(m, h):
+            if ("sq", m) not in st:
+                sq = wk.tile([P, 2], F32, name="sq", bufs=2)
+                st["sq", m] = sq
+            junk = wk.tile([P, 512], BF16, name="junk", bufs=2)
+            nc.scalar.activation(
+                out=junk[:], in_=st["c", m, h][:], func=ACTF.Square,
+                accum_out=st["sq", m][:, h : h + 1],
+            )
+
+        def read_norm(m):
+            sq = st["sq", m]
+            tot = wk.tile([P, 1], F32, name="tot", bufs=2)
+            nc.gpsimd.tensor_tensor(out=tot[:], in0=sq[:, 0:1], in1=sq[:, 1:2], op=ALU.add)
+            ms = wk.tile([P, 1], F32, name="ms", bufs=2)
+            nc.gpsimd.tensor_scalar(
+                out=ms[:], in0=tot[:], scalar1=1.0 / D, scalar2=EPS, op0=ALU.mult, op1=ALU.add
+            )
+            rstd = wk.tile([P, 1], F32, name="rstd", bufs=2)
+            nc.gpsimd.tensor_tensor(out=rstd[:], in0=ms[:], in1=mhalf[:], op=ALU.pow)
+            st["rstd", m] = rstd
+
+        def read_out(m, h):
+            last = ("yt", m) in st
+            if not last:
+                yt = wk.tile([P, D], F32, name="yt", bufs=2)
+                st["yt", m] = yt
+            yt = st["yt", m]
+            nc.vector.scalar_tensor_tensor(
+                out=yt[:, 512 * h : 512 * (h + 1)], in0=st["c", m, h][:],
+                scalar=st["rstd", m][:], in1=gn[:, 512 * h : 512 * (h + 1)],
+                op0=ALU.mult, op1=ALU.mult,
+            )
+            if last:
+                nc.sync.dma_start(out=out_0[P * m : P * (m + 1), :], in_=yt[:])
+
+        def decay_product(n, h):
+            s, a = divmod(n, 4)
+            sb = ps.tile([P, 512], F32, name="sd", bufs=SDB)
+            nc.tensor.matmul_mx(
+                out=sb[:],
+                lhsT=selq[:, P * a : P * (a + 1)].bitcast(FP8X4),
+                lhsT_scale=sels[:, P * a : P * (a + 1)],
+                rhs=sw[:, s, 2048 * h : 2048 * (h + 1)].bitcast(FP8X4),
+                rhs_scale=ssc[:, s, 512 * h : 512 * (h + 1)],
+                start=True,
+                stop=True,
+            )
+            st["s", n, h] = sb
+
+        def decay_scale(n, h):
+            kst = wk.tile([P, 512], F32, name="kst", bufs=KSB)
+            nc.scalar.activation(
+                out=kst[:], in_=st["s", n, h][:], func=ACTF.Copy, scale=keepn[:, n : n + 1]
+            )
+            st["kst", n, h] = kst
+
+        def update_product(n, h):
+            s, a = divmod(n, 4)
+            cols = slice(512 * s + P * a, 512 * s + P * (a + 1))
+            db = ps.tile([P, 512], F32, name="sd", bufs=SDB)
+            for g in range(TG):
+                nc.tensor.matmul_mx(
+                    out=db[:],
+                    lhsT=pkq[g][:, cols].bitcast(FP8X4),
+                    lhsT_scale=pks[g][:, cols],
+                    rhs=vq[g][:, 512 * h : 512 * (h + 1)].bitcast(FP8X4),
+                    rhs_scale=vsc[g][:, 512 * h : 512 * (h + 1)],
+                    start=(g == 0),
+                    stop=(g == TG - 1),
+                )
+            st["d", n, h] = db
+
+        def update_add(n, h):
+            last = ("nt", n) in st
+            if not last:
+                nt = wk.tile([P, D], F32, name="nt", bufs=2)
+                st["nt", n] = nt
+            nt = st["nt", n]
+            nc.vector.tensor_tensor(
+                out=nt[:, 512 * h : 512 * (h + 1)], in0=st["d", n, h][:],
+                in1=st["kst", n, h][:], op=ALU.add,
+            )
+            if last:
+                nc.sync.dma_start(out=out_1[P * n : P * (n + 1), :], in_=nt[:])
+
+        def sel_quantize():
+            nc.vector.quantize_mx(
+                out=selq[:].bitcast(FP8X4), scales=sels[:], in_=sel[:].rearrange("p f t -> p (f t)")
+            )
+
+        def sign_and_scale():
+            wflat = wr[:].rearrange("p g t -> p (g t)")
+            wlt = cst.tile([P, TG * 4], F32, name="wlt")
+            nc.vector.tensor_scalar(out=wlt[:], in0=wflat, scalar1=0.0, scalar2=None, op0=ALU.is_lt)
+            wsgn = cst.tile([P, TG * 4], F32, name="wsgn")
+            nc.vector.scalar_tensor_tensor(
+                out=wsgn[:], in0=wflat, scalar=0.0, in1=wlt[:], op0=ALU.is_gt, op1=ALU.subtract,
+            )
+            nc.vector.tensor_tensor(
+                out=vss[:], in0=vs[:].rearrange("p g t -> p (g t)"), in1=wsgn[:], op=ALU.mult
+            )
+
+        def write_abs():
+            wflat = wr[:].rearrange("p g t -> p (g t)")
+            wneg = cst.tile([P, TG * 4], F32, name="wneg")
+            nc.vector.tensor_scalar(out=wneg[:], in0=wflat, scalar1=-1.0, scalar2=None, op0=ALU.mult)
+            wabs = cst.tile([P, TG * 4], F32, name="wabs")
+            nc.vector.tensor_tensor(out=wabs[:], in0=wflat, in1=wneg[:], op=ALU.max)
+            wroot = cst.tile([P, TG * 4], F32, name="wroot")
+            nc.gpsimd.tensor_tensor(out=wroot[:], in0=wabs[:], in1=quarter[:], op=ALU.pow)
+            st["wroot"] = wroot
+
+        def write_clip():
+            wclip = cst.tile([P, TG * 4], F32, name="wclip")
+            nc.vector.tensor_scalar(
+                out=wclip[:], in0=st["wroot"][:], scalar1=1e-11, scalar2=None, op0=ALU.max
+            )
+            st["wclip"] = wclip
+
+        def write_ln():
+            wln = cst.tile([P, TG * 4], F32, name="wln")
+            nc.scalar.activation(out=wln[:], in_=st["wclip"][:], func=ACTF.Ln)
+            st["wln"] = wln
+
+        def write_bias():
+            nc.vector.scalar_tensor_tensor(
+                out=kbias[:], in0=st["wln"][:], scalar=4.0, in1=hn[:].rearrange("p g t -> p (g t)"),
+                op0=ALU.mult, op1=ALU.subtract,
+            )
+
+
+        transposes(0)
+        sign_and_scale()
+        write_abs()
+        copy_out(0)
+        quantize_rows(0)
+        transposes(1)
+        write_clip()
+        widen(3)
+        write_ln()
+        copy_out(1)
+        widen(0)
+        transposes(2)
+        widen(2)
+        widen(1)
+        copy_out(2)
+        write_bias()
+        quantize_rows(1)
+        transposes(3)
+        values_interleave(0, 0)
+        widen(4)
+        copy_out(3)
+        values_interleave(0, 1)
+        widen(5)
+        transposes(4)
+        key_product(0)
+        permute_scales(0)
+        copy_out(4)
+        key_product(1)
+        values_quantize(0)
+        key_exp(0, 1)
+        transposes(5)
+        key_exp(1, 1)
+        permute_scales(1)
+        key_exp(0, 0)
+        widen(7)
+        key_exp(1, 0)
+        permute_omega(1)
+        widen(8)
+        quantize_rows(2)
+        widen(6)
+        keep_columns()
+        widen(11)
+        key_product(2)
+        quantize_rows(3)
+        quantize_rows(4)
+        copy_out(5)
+        key_product(3)
+        values_interleave(1, 0)
+        key_exp(2, 1)
+        transposes(6)
+        key_exp(3, 0)
+        values_interleave(1, 1)
+        copy_out(6)
+        key_exp(3, 1)
+        transposes(7)
+        quantize_rows(5)
+        key_exp(2, 0)
+        keep_turn()
+        values_quantize(1)
+        copy_out(7)
+        key_product(4)
+        widen(10)
+        features_interleave(0, 0)
+        transposes(8)
+        key_exp(4, 0)
+        quantize_rows(6)
+        copy_out(8)
+        features_interleave(0, 1)
+        key_exp(4, 1)
+        transposes(9)
+        widen(9)
+        key_product(5)
+        quantize_rows(7)
+        permute_omega(0)
+        copy_out(9)
+        key_exp(5, 1)
+        features_quantize(0, 0)
+        transposes(10)
+        key_exp(5, 0)
+        keep_copy()
+        sel_quantize()
+        key_product(6)
+        copy_out(10)
+        quantize_rows(8)
+        key_product(7)
+        values_interleave(2, 0)
+        key_exp(6, 0)
+        transposes(11)
+        key_exp(6, 1)
+        decay_product(0, 0)
+        key_exp(7, 1)
+        quantize_rows(9)
+        decay_product(0, 1)
+        quantize_rows(10)
+        key_product(8)
+        copy_out(11)
+        features_quantize(0, 1)
+        decay_product(1, 0)
+        key_exp(7, 0)
+        quantize_rows(11)
+        transposes(12)
+        values_interleave(2, 1)
+        key_exp(8, 1)
+        key_product(9)
+        copy_out(12)
+        features_interleave(1, 0)
+        key_exp(8, 0)
+        transposes(13)
+        key_exp(9, 0)
+        key_product(10)
+        copy_out(13)
+        features_interleave(1, 1)
+        key_exp(10, 1)
+        transposes(14)
+        key_exp(10, 0)
+        values_quantize(2)
+        copy_out(14)
+        key_product(11)
+        key_exp(9, 1)
+        quantize_rows(12)
+        transposes(15)
+        key_exp(11, 0)
+        features_quantize(1, 0)
+        query_product(0)
+        copy_out(15)
+        features_quantize(1, 1)
+        key_exp(11, 1)
+        features_interleave(2, 0)
+        transposes(16)
+        query_exp(0, 0)
+        query_exp(0, 1)
+        features_interleave(2, 1)
+        decay_scale(0, 0)
+        decay_scale(0, 1)
+        decay_product(1, 1)
+        quantize_rows(13)
+        decay_scale(1, 0)
+        decay_product(2, 0)
+        features_quantize(2, 0)
+        query_product(1)
+        copy_out(16)
+        query_scale(0)
+        decay_product(2, 1)
+        decay_scale(1, 1)
+        transposes(17)
+        query_exp(1, 1)
+        quantize_rows(14)
+        update_product(0, 0)
+        query_quantize(0)
+        query_exp(1, 0)
+        quantize_rows(15)
+        features_quantize(2, 1)
+        copy_out(17)
+        read_product(0, 0)
+        query_scale(1)
+        read_product(0, 1)
+        read_square(0, 0)
+        query_product(2)
+        read_square(0, 1)
+        update_add(0, 0)
+        query_product(3)
+        query_exp(2, 0)
+        read_norm(0)
+        query_quantize(1)
+        quantize_rows(16)
+        transposes(18)
+        query_exp(2, 1)
+        quantize_rows(17)
+        read_out(0, 0)
+        query_exp(3, 0)
+        update_product(0, 1)
+        read_out(0, 1)
+        decay_scale(2, 0)
+        read_product(1, 0)
+        query_scale(2)
+        query_exp(3, 1)
+        read_product(1, 1)
+        copy_out(18)
+        query_product(4)
+        update_add(0, 1)
+        read_square(1, 0)
+        query_quantize(2)
+        transposes(19)
+        read_square(1, 1)
+        query_scale(3)
+        query_exp(4, 0)
+        decay_product(3, 0)
+        read_norm(1)
+        decay_product(3, 1)
+        query_exp(4, 1)
+        query_product(5)
+        quantize_rows(18)
+        query_quantize(3)
+        decay_scale(2, 1)
+        query_product(6)
+        read_out(1, 0)
+        query_exp(5, 1)
+        update_product(1, 0)
+        read_out(1, 1)
+        query_exp(5, 0)
+        query_scale(4)
+        read_product(2, 0)
+        copy_out(19)
+        read_product(2, 1)
+        read_square(2, 0)
+        update_add(1, 0)
+        read_square(2, 1)
+        query_quantize(4)
+        update_product(1, 1)
+        query_scale(5)
+        decay_scale(3, 0)
+        read_norm(2)
+        query_exp(6, 1)
+        update_product(2, 0)
+        update_add(1, 1)
+        query_exp(6, 0)
+        read_out(2, 0)
+        update_product(2, 1)
+        decay_scale(3, 1)
+        read_out(2, 1)
+        read_product(3, 0)
+        update_add(2, 0)
+        read_product(3, 1)
+        update_add(2, 1)
+        read_square(3, 0)
+        decay_product(4, 0)
+        query_quantize(5)
+        read_square(3, 1)
+        decay_product(4, 1)
+        quantize_rows(19)
+        update_product(3, 0)
+        query_scale(6)
+        decay_scale(4, 0)
+        read_norm(3)
+        decay_scale(4, 1)
+        query_product(7)
+        update_add(3, 0)
+        update_product(3, 1)
+        query_exp(7, 1)
+        read_out(3, 1)
+        query_exp(7, 0)
+        decay_product(5, 0)
+        read_out(3, 0)
+        read_product(4, 0)
+        decay_scale(5, 0)
+        update_add(3, 1)
+        read_product(4, 1)
+        read_square(4, 0)
+        query_scale(7)
+        decay_product(5, 1)
+        read_square(4, 1)
+        update_product(4, 0)
+        decay_scale(5, 1)
+        read_norm(4)
+        query_quantize(6)
+        update_product(4, 1)
+        update_add(4, 0)
+        read_out(4, 1)
+        decay_product(6, 0)
+        decay_product(6, 1)
+        decay_scale(6, 0)
+        read_out(4, 0)
+        read_product(5, 0)
+        update_add(4, 1)
+        read_product(5, 1)
+        read_square(5, 0)
+        update_product(5, 0)
+        query_quantize(7)
+        read_square(5, 1)
+        decay_scale(6, 1)
+        update_product(5, 1)
+        read_norm(5)
+        update_add(5, 0)
+        decay_product(7, 0)
+        read_out(5, 0)
+        decay_product(7, 1)
+        decay_scale(7, 0)
+        read_out(5, 1)
+        read_product(6, 0)
+        update_add(5, 1)
+        read_product(6, 1)
+        read_square(6, 0)
+        update_product(6, 0)
+        read_square(6, 1)
+        decay_scale(7, 1)
+        update_product(6, 1)
+        read_norm(6)
+        update_add(6, 0)
+        update_product(7, 0)
+        read_out(6, 0)
+        update_add(6, 1)
+        update_product(7, 1)
+        read_out(6, 1)
+        read_product(7, 0)
+        read_product(7, 1)
+        update_add(7, 1)
+        read_square(7, 0)
+        update_add(7, 0)
+        read_square(7, 1)
+        read_norm(7)
+        read_out(7, 1)
+        read_out(7, 0)

@@ -19,7 +19,8 @@ M, T, K, R, F, D = 1024, 1536, 1024, 512, 1024, 1024
 EPS = 1e-6
 FLOPS = 2 * (M * K * R + T * K * R + M * F * D + T * F * D)
 
-TPB, ABB, CB, SDB, KSB = 1,2,2,3,4
+TPB, ABB, CB, SDB = 1,2,2,3
+UPDATE_ON_VECTOR = ()
 KG = K // 512
 TG = T // 512
 FG = F // 512
@@ -60,14 +61,16 @@ def tile_performer_state_step_f7_kernel(
         hn = cst.tile([P, TG, 4], BF16, name="hn")
         vs = cst.tile([P, TG, 4], F32, name="vs")
         rd = cst.tile([P, FG, 4], BF16, name="rd")
-        kz = cst.tile([P, P], BF16, name="kz")
+        kk = cst.tile([P, 2, 2, 4], BF16, name="kk")
+        sd = cst.tile([P, FG, 2, 4 * D], U8, name="sd", align_bytes=64)
+        sds = cst.tile([P, FG, 2, D], U8, name="sds", align_bytes=64)
         gn = cst.tile([P, D], BF16, name="gn")
 
         nc.gpsimd.memset(osc[:].bitcast(I32), 0)
         identf = cst.tile([P, P], F32, name="identf")
         make_identity(nc, identf[:])
-        nc.gpsimd.memset(kz[:], 0.0)
         nc.gpsimd.memset(ssc[:].bitcast(I32), 0)
+        nc.gpsimd.memset(sds[:].rearrange("p s j n -> p (s j n)").bitcast(I32), 0)
 
         vview = values_bytes.rearrange("(g p t) d -> g p t d", p=P, t=4)
         oview = omega_scales.rearrange("g (q r) n -> r q g n", r=4)
@@ -87,7 +90,9 @@ def tile_performer_state_step_f7_kernel(
         for t in range(4):
             nc.sync.dma_start(out=kraw[4 + t][:], in_=kview[1, t])
         nc.sync.dma_start(out=rd[:], in_=read.rearrange("(g p t) -> p g t", p=P, t=4))
-        nc.sync.dma_start(out=kz[0:8, :], in_=keep.rearrange("(c p) -> c p", p=P))
+        kview4 = keep.rearrange("(s j b r t) -> b r s j t", s=2, j=2, b=2, r=32)
+        for q in range(4):
+            nc.sync.dma_start(out=kk[32 * q : 32 * (q + 1)], in_=kview4[q // 2])
         nc.sync.dma_start(out=vbytes[2][:], in_=vview[2])
         for t in range(4):
             nc.sync.dma_start(out=kraw[8 + t][:], in_=kview[2, t])
@@ -96,6 +101,18 @@ def tile_performer_state_step_f7_kernel(
             nc.sync.dma_start(out=ssc[r:P:32, :, :].bitcast(I32), in_=sview[r].bitcast(I32))
         for m in range(8):
             nc.sync.dma_start(out=qraw[m][:], in_=queries[P * m : P * (m + 1), :])
+        wview = state_words.rearrange("s (j b r) n t -> s j b r (n t)", j=2, b=2)
+        for s in range(FG):
+            for j in range(2):
+                for q in range(4):
+                    nc.sync.dma_start(
+                        out=sd[32 * q : 32 * (q + 1), s, j].bitcast(I32), in_=wview[s, j, q // 2].bitcast(I32)
+                    )
+        for q in range(4):
+            nc.sync.dma_start(
+                out=sds[32 * q : 32 * q + 4].bitcast(I32),
+                in_=state_scales.rearrange("s (j b r) n -> b r s j n", j=2, b=2)[q // 2].bitcast(I32),
+            )
         nc.sync.dma_start(out=gn[:], in_=gain.partition_broadcast(P))
 
         quarter = cst.tile([P, TG * 4], F32, name="quarter")
@@ -105,18 +122,16 @@ def tile_performer_state_step_f7_kernel(
         kbias = cst.tile([P, TG * 4], F32, name="kbias")
         vss = cst.tile([P, TG * 4], F32, name="vss")
 
-        sel = cst.tile([P, 512, 4], BF16, name="sel", align_bytes=64)
-        nc.gpsimd.memset(sel[:].rearrange("p f t -> p (f t)"), 0.0)
-        nc.gpsimd.affine_select(
-            out=sel[:], in_=sel[:], compare_op=ALU.not_equal, fill=1.0, base=0,
-            pattern=[[1, 512], [-1, 4]], channel_multiplier=-4,
-        )
-        selq = cst.tile([P, 512], U32, name="selq", align_bytes=64)
-        sels = cst.tile([P, 512], U8, name="sels", align_bytes=64)
+        klow = cst.tile([P, 2, 2, 4], BF16, name="klow")
+        mask = cst.tile([P, 8], I32, name="mask")
+        eye = cst.tile([P, 32], BF16, name="eye")
+        dk = cst.tile([P, 4, 32, 16], BF16, name="dk", align_bytes=64)
+        dcod = cst.tile([P, 4 * P], U32, name="dcod", align_bytes=64)
+        dsc = cst.tile([P, 4 * P], U8, name="dsc", align_bytes=64)
+        dz = cst.tile([P, 2, 4 * P], U32, name="dz", align_bytes=64)
 
         owp = cst.tile([P, KG, 4, P, 2], U8, name="owp", align_bytes=64)
         osp = cst.tile([P, KG, 4, P], U8, name="osp", align_bytes=64)
-        keepn = cst.tile([P, 8], F32, name="keepn")
         pkq, pks, vq, vsc = [], [], [], []
         for g in range(TG):
             a = cst.tile([P, F], U32, name=f"pkq{g}", align_bytes=64)
@@ -214,7 +229,7 @@ def tile_performer_state_step_f7_kernel(
             )
 
         def features_interleave(g, s):
-            pint = wk.tile([P, R * 4], BF16, name="pint", align_bytes=64)
+            pint = wk.tile([P, R * 4], BF16, name="pint", bufs=2, align_bytes=64)
             interleave(pint[:], st["pl", g][:, s])
             st["pint", g, s] = pint
 
@@ -234,20 +249,6 @@ def tile_performer_state_step_f7_kernel(
             nc.vector.tensor_copy(
                 out=osp[:, c], in_=osc[:, c].rearrange("p (m t) -> p t m", t=4)
             )
-
-        def keep_columns():
-            kzf = cst.tile([P, P], F32, name="kzf")
-            nc.vector.tensor_copy(out=kzf[:], in_=kz[:])
-            st["kzf"] = kzf
-
-        def keep_turn():
-            kt = ps.tile([P, P], F32, name="ab", bufs=ABB)
-            nc.tensor.transpose(kt[:], st["kzf"][:], identf[:])
-            st["kt"] = kt
-
-        def keep_copy():
-            kt = st["kt"]
-            nc.vector.tensor_copy(out=keepn[:], in_=kt[:, 0:8])
 
         def query_product(m):
             qq, qs = st["xq", 12 + m]
@@ -312,17 +313,15 @@ def tile_performer_state_step_f7_kernel(
                 st["sq", m] = sq
             junk = wk.tile([P, 512], BF16, name="junk", bufs=2)
             nc.scalar.activation(
-                out=junk[:], in_=st["c", m, h][:], func=ACTF.Square,
+                out=junk[:], in_=st["c", m, h][:], func=ACTF.Square, scale=1.0 / 32.0,
                 accum_out=st["sq", m][:, h : h + 1],
             )
 
         def read_norm(m):
             sq = st["sq", m]
-            tot = wk.tile([P, 1], F32, name="tot", bufs=2)
-            nc.gpsimd.tensor_tensor(out=tot[:], in0=sq[:, 0:1], in1=sq[:, 1:2], op=ALU.add)
             ms = wk.tile([P, 1], F32, name="ms", bufs=2)
             nc.gpsimd.tensor_scalar(
-                out=ms[:], in0=tot[:], scalar1=1.0 / D, scalar2=EPS, op0=ALU.mult, op1=ALU.add
+                out=ms[:], in0=sq[:, 0:1], scalar1=sq[:, 1:2], scalar2=EPS, op0=ALU.add, op1=ALU.add
             )
             rstd = wk.tile([P, 1], F32, name="rstd", bufs=2)
             nc.gpsimd.tensor_tensor(out=rstd[:], in0=ms[:], in1=mhalf[:], op=ALU.pow)
@@ -342,60 +341,90 @@ def tile_performer_state_step_f7_kernel(
             if last:
                 nc.sync.dma_start(out=out_0[P * m : P * (m + 1), :], in_=yt[:])
 
-        def decay_product(n, h):
+        def decay_eye():
+            half = wk.tile([P, 64], F32, name="half", bufs=1)
+            nc.gpsimd.tensor_tensor(out=half[:], in0=identf[:, 0:64], in1=identf[:, 64:128], op=ALU.add)
+            nc.gpsimd.tensor_tensor(out=eye[:], in0=half[:, 0:32], in1=half[:, 32:64], op=ALU.add)
+
+        def decay_zero():
+            nc.gpsimd.memset(dz[:].bitcast(I32), 0)
+            nc.gpsimd.memset(dk[:].rearrange("p c r x -> p (c r x)"), 0.0)
+            nc.gpsimd.memset(mask[:], -983056)
+
+        def decay_split():
+            flat = kk[:].rearrange("p s j t -> p (s j t)")
+            khi = cst.tile([P, 16], BF16, name="khi")
+            nc.vector.tensor_tensor(
+                out=khi[:].bitcast(I32), in0=flat.bitcast(I32), in1=mask[:], op=ALU.bitwise_and
+            )
+            low = klow[:].rearrange("p s j t -> p (s j t)")
+            nc.vector.tensor_tensor(out=low, in0=flat, in1=khi[:], op=ALU.subtract)
+            for q in (0, 2):
+                nc.vector.tensor_copy(
+                    out=low[32 * q : 32 * (q + 1)], in_=khi[32 * q : 32 * (q + 1), :]
+                )
+
+        def decay_build():
+            nc.vector.tensor_tensor(
+                out=dk[:, :, :, 0:16:5],
+                in0=eye[:].unsqueeze(1).unsqueeze(3).to_broadcast([P, 4, 32, 4]),
+                in1=klow[:].rearrange("p s j t -> p (s j) t").unsqueeze(2).to_broadcast([P, 4, 32, 4]),
+                op=ALU.mult,
+            )
+
+        def decay_quantize():
+            nc.vector.quantize_mx(
+                out=dcod[:].bitcast(FP8X4), scales=dsc[:], in_=dk[:].rearrange("p c r x -> p (c r x)")
+            )
+
+        def decay_place():
+            for b in range(2):
+                nc.vector.tensor_copy(
+                    out=dz[64 * b : 64 * (b + 1), b, :].bitcast(I32),
+                    in_=dcod[64 * b : 64 * (b + 1), :].bitcast(I32),
+                )
+
+        def update_start(n, h):
             s, a = divmod(n, 4)
-            sb = ps.tile([P, 512], F32, name="sd", bufs=SDB)
+            j, b = divmod(a, 2)
+            db = ps.tile([P, 512], F32, name="sd", bufs=SDB)
+            st["d", n, h] = db
+            cols = slice(P * (2 * s + j), P * (2 * s + j + 1))
             nc.tensor.matmul_mx(
-                out=sb[:],
-                lhsT=selq[:, P * a : P * (a + 1)].bitcast(FP8X4),
-                lhsT_scale=sels[:, P * a : P * (a + 1)],
-                rhs=sw[:, s, 2048 * h : 2048 * (h + 1)].bitcast(FP8X4),
-                rhs_scale=ssc[:, s, 512 * h : 512 * (h + 1)],
+                out=db[:],
+                lhsT=dz[:, b, cols].bitcast(FP8X4),
+                lhsT_scale=dsc[:, cols],
+                rhs=sd[:, s, j, 2048 * h : 2048 * (h + 1)].bitcast(FP8X4),
+                rhs_scale=sds[:, s, j, 512 * h : 512 * (h + 1)],
                 start=True,
-                stop=True,
+                stop=False,
             )
-            st["s", n, h] = sb
 
-        def decay_scale(n, h):
-            kst = wk.tile([P, 512], F32, name="kst", bufs=KSB)
-            nc.scalar.activation(
-                out=kst[:], in_=st["s", n, h][:], func=ACTF.Copy, scale=keepn[:, n : n + 1]
-            )
-            st["kst", n, h] = kst
-
-        def update_product(n, h):
+        def update_add(n, h, g):
             s, a = divmod(n, 4)
             cols = slice(512 * s + P * a, 512 * s + P * (a + 1))
-            db = ps.tile([P, 512], F32, name="sd", bufs=SDB)
-            for g in range(TG):
-                nc.tensor.matmul_mx(
-                    out=db[:],
-                    lhsT=pkq[g][:, cols].bitcast(FP8X4),
-                    lhsT_scale=pks[g][:, cols],
-                    rhs=vq[g][:, 512 * h : 512 * (h + 1)].bitcast(FP8X4),
-                    rhs_scale=vsc[g][:, 512 * h : 512 * (h + 1)],
-                    start=(g == 0),
-                    stop=(g == TG - 1),
-                )
-            st["d", n, h] = db
+            nc.tensor.matmul_mx(
+                out=st["d", n, h][:],
+                lhsT=pkq[g][:, cols].bitcast(FP8X4),
+                lhsT_scale=pks[g][:, cols],
+                rhs=vq[g][:, 512 * h : 512 * (h + 1)].bitcast(FP8X4),
+                rhs_scale=vsc[g][:, 512 * h : 512 * (h + 1)],
+                start=False,
+                stop=(g == TG - 1),
+            )
 
-        def update_add(n, h):
+        def update_out(n, h):
             last = ("nt", n) in st
             if not last:
                 nt = wk.tile([P, D], F32, name="nt", bufs=2)
                 st["nt", n] = nt
             nt = st["nt", n]
-            nc.vector.tensor_tensor(
-                out=nt[:, 512 * h : 512 * (h + 1)], in0=st["d", n, h][:],
-                in1=st["kst", n, h][:], op=ALU.add,
-            )
+            if (n, h) in UPDATE_ON_VECTOR:
+                nc.vector.tensor_copy(out=nt[:, 512 * h : 512 * (h + 1)], in_=st["d", n, h][:])
+            else:
+                nc.scalar.copy(out=nt[:, 512 * h : 512 * (h + 1)], in_=st["d", n, h][:])
             if last:
                 nc.sync.dma_start(out=out_1[P * n : P * (n + 1), :], in_=nt[:])
-
-        def sel_quantize():
-            nc.vector.quantize_mx(
-                out=selq[:].bitcast(FP8X4), scales=sels[:], in_=sel[:].rearrange("p f t -> p (f t)")
-            )
 
         def sign_and_scale():
             wflat = wr[:].rearrange("p g t -> p (g t)")
@@ -438,305 +467,323 @@ def tile_performer_state_step_f7_kernel(
             )
 
 
+        decay_zero()
         transposes(0)
         sign_and_scale()
+        decay_eye()
         write_abs()
         copy_out(0)
+        write_clip()
+        write_ln()
         quantize_rows(0)
         transposes(1)
-        write_clip()
-        widen(3)
-        write_ln()
-        copy_out(1)
-        widen(0)
-        transposes(2)
         widen(2)
+        copy_out(1)
+        widen(3)
         widen(1)
-        copy_out(2)
+        transposes(2)
         write_bias()
         quantize_rows(1)
+        copy_out(2)
+        widen(0)
         transposes(3)
-        values_interleave(0, 0)
+        quantize_rows(2)
         widen(4)
+        values_interleave(0, 0)
         copy_out(3)
-        values_interleave(0, 1)
-        widen(5)
-        transposes(4)
         key_product(0)
-        permute_scales(0)
-        copy_out(4)
-        key_product(1)
-        values_quantize(0)
-        key_exp(0, 1)
-        transposes(5)
-        key_exp(1, 1)
         permute_scales(1)
+        widen(5)
+        key_product(1)
+        permute_scales(0)
+        transposes(4)
+        decay_split()
+        quantize_rows(3)
+        key_exp(1, 1)
+        values_interleave(0, 1)
         key_exp(0, 0)
-        widen(7)
         key_exp(1, 0)
         permute_omega(1)
-        widen(8)
-        quantize_rows(2)
-        widen(6)
-        keep_columns()
-        widen(11)
+        key_exp(0, 1)
         key_product(2)
-        quantize_rows(3)
-        quantize_rows(4)
-        copy_out(5)
-        key_product(3)
-        values_interleave(1, 0)
-        key_exp(2, 1)
-        transposes(6)
-        key_exp(3, 0)
-        values_interleave(1, 1)
-        copy_out(6)
-        key_exp(3, 1)
-        transposes(7)
-        quantize_rows(5)
-        key_exp(2, 0)
-        keep_turn()
-        values_quantize(1)
-        copy_out(7)
-        key_product(4)
-        widen(10)
-        features_interleave(0, 0)
-        transposes(8)
-        key_exp(4, 0)
-        quantize_rows(6)
-        copy_out(8)
-        features_interleave(0, 1)
-        key_exp(4, 1)
-        transposes(9)
         widen(9)
-        key_product(5)
-        quantize_rows(7)
+        key_product(3)
+        values_quantize(0)
+        key_exp(3, 0)
+        widen(7)
+        key_exp(2, 0)
         permute_omega(0)
-        copy_out(9)
-        key_exp(5, 1)
+        key_exp(2, 1)
+        key_exp(3, 1)
+        features_interleave(0, 0)
+        widen(8)
+        features_interleave(0, 1)
+        copy_out(4)
+        widen(6)
+        transposes(5)
+        quantize_rows(4)
         features_quantize(0, 0)
-        transposes(10)
+        copy_out(5)
+        key_product(4)
+        values_interleave(1, 0)
+        widen(10)
+        transposes(6)
+        key_exp(4, 1)
+        quantize_rows(5)
+        values_interleave(1, 1)
+        key_exp(4, 0)
+        key_product(5)
+        copy_out(6)
         key_exp(5, 0)
-        keep_copy()
-        sel_quantize()
-        key_product(6)
-        copy_out(10)
-        quantize_rows(8)
-        key_product(7)
+        widen(11)
+        transposes(7)
+        quantize_rows(6)
+        key_exp(5, 1)
         values_interleave(2, 0)
-        key_exp(6, 0)
-        transposes(11)
+        key_product(6)
+        copy_out(7)
         key_exp(6, 1)
-        decay_product(0, 0)
-        key_exp(7, 1)
-        quantize_rows(9)
-        decay_product(0, 1)
-        quantize_rows(10)
-        key_product(8)
-        copy_out(11)
+        transposes(8)
+        quantize_rows(7)
         features_quantize(0, 1)
-        decay_product(1, 0)
+        key_exp(6, 0)
+        key_product(7)
+        values_quantize(1)
+        copy_out(8)
         key_exp(7, 0)
-        quantize_rows(11)
-        transposes(12)
-        values_interleave(2, 1)
-        key_exp(8, 1)
-        key_product(9)
-        copy_out(12)
+        transposes(9)
+        key_exp(7, 1)
+        quantize_rows(8)
         features_interleave(1, 0)
+        copy_out(9)
+        key_product(8)
+        key_exp(8, 1)
+        transposes(10)
+        quantize_rows(9)
+        features_interleave(1, 1)
         key_exp(8, 0)
-        transposes(13)
+        key_product(9)
+        copy_out(10)
+        key_exp(9, 1)
+        quantize_rows(10)
+        transposes(11)
+        values_interleave(2, 1)
         key_exp(9, 0)
         key_product(10)
-        copy_out(13)
-        features_interleave(1, 1)
+        copy_out(11)
         key_exp(10, 1)
-        transposes(14)
-        key_exp(10, 0)
+        quantize_rows(11)
+        transposes(12)
         values_quantize(2)
-        copy_out(14)
+        key_exp(10, 0)
         key_product(11)
-        key_exp(9, 1)
-        quantize_rows(12)
-        transposes(15)
-        key_exp(11, 0)
-        features_quantize(1, 0)
-        query_product(0)
-        copy_out(15)
-        features_quantize(1, 1)
+        copy_out(12)
+        decay_build()
         key_exp(11, 1)
-        features_interleave(2, 0)
-        transposes(16)
+        quantize_rows(12)
+        transposes(13)
+        decay_quantize()
+        key_exp(11, 0)
+        query_product(0)
+        features_quantize(1, 1)
+        copy_out(13)
+        decay_place()
         query_exp(0, 0)
-        query_exp(0, 1)
-        features_interleave(2, 1)
-        decay_scale(0, 0)
-        decay_scale(0, 1)
-        decay_product(1, 1)
+        transposes(14)
         quantize_rows(13)
-        decay_scale(1, 0)
-        decay_product(2, 0)
-        features_quantize(2, 0)
+        query_exp(0, 1)
+        features_interleave(2, 0)
         query_product(1)
-        copy_out(16)
-        query_scale(0)
-        decay_product(2, 1)
-        decay_scale(1, 1)
-        transposes(17)
-        query_exp(1, 1)
-        quantize_rows(14)
-        update_product(0, 0)
-        query_quantize(0)
+        copy_out(14)
+        update_start(0, 0)
         query_exp(1, 0)
-        quantize_rows(15)
-        features_quantize(2, 1)
-        copy_out(17)
-        read_product(0, 0)
+        transposes(15)
+        query_scale(0)
+        query_exp(1, 1)
+        update_add(0, 0, 0)
+        copy_out(15)
+        update_start(0, 1)
+        update_add(0, 1, 0)
         query_scale(1)
-        read_product(0, 1)
-        read_square(0, 0)
-        query_product(2)
-        read_square(0, 1)
-        update_add(0, 0)
-        query_product(3)
-        query_exp(2, 0)
-        read_norm(0)
+        update_start(1, 0)
+        transposes(16)
+        query_quantize(0)
+        update_add(1, 0, 0)
+        copy_out(16)
         query_quantize(1)
-        quantize_rows(16)
-        transposes(18)
-        query_exp(2, 1)
-        quantize_rows(17)
-        read_out(0, 0)
-        query_exp(3, 0)
-        update_product(0, 1)
+        read_product(0, 0)
+        quantize_rows(14)
+        quantize_rows(15)
+        read_product(0, 1)
+        features_quantize(1, 0)
+        read_square(0, 0)
+        transposes(17)
+        features_quantize(2, 0)
+        read_square(0, 1)
+        query_product(2)
+        features_interleave(2, 1)
+        copy_out(17)
+        read_norm(0)
+        update_add(1, 0, 1)
+        query_exp(2, 0)
+        update_add(0, 1, 1)
+        update_add(0, 1, 2)
         read_out(0, 1)
-        decay_scale(2, 0)
+        query_exp(2, 1)
+        transposes(18)
+        read_out(0, 0)
+        update_out(0, 1)
         read_product(1, 0)
-        query_scale(2)
-        query_exp(3, 1)
-        read_product(1, 1)
+        features_quantize(2, 1)
         copy_out(18)
-        query_product(4)
-        update_add(0, 1)
+        read_product(1, 1)
         read_square(1, 0)
+        query_scale(2)
+        update_add(0, 0, 1)
+        read_square(1, 1)
+        update_add(0, 0, 2)
+        query_product(3)
+        quantize_rows(16)
+        update_out(0, 0)
+        read_norm(1)
         query_quantize(2)
         transposes(19)
-        read_square(1, 1)
-        query_scale(3)
-        query_exp(4, 0)
-        decay_product(3, 0)
-        read_norm(1)
-        decay_product(3, 1)
-        query_exp(4, 1)
-        query_product(5)
-        quantize_rows(18)
-        query_quantize(3)
-        decay_scale(2, 1)
-        query_product(6)
-        read_out(1, 0)
-        query_exp(5, 1)
-        update_product(1, 0)
+        query_exp(3, 1)
+        quantize_rows(17)
         read_out(1, 1)
-        query_exp(5, 0)
-        query_scale(4)
+        update_add(1, 0, 2)
+        query_exp(3, 0)
+        query_product(4)
+        read_out(1, 0)
+        update_out(1, 0)
+        query_scale(3)
         read_product(2, 0)
         copy_out(19)
         read_product(2, 1)
+        query_exp(4, 1)
+        quantize_rows(18)
+        query_product(5)
         read_square(2, 0)
-        update_add(1, 0)
-        read_square(2, 1)
-        query_quantize(4)
-        update_product(1, 1)
-        query_scale(5)
-        decay_scale(3, 0)
-        read_norm(2)
-        query_exp(6, 1)
-        update_product(2, 0)
-        update_add(1, 1)
-        query_exp(6, 0)
-        read_out(2, 0)
-        update_product(2, 1)
-        decay_scale(3, 1)
-        read_out(2, 1)
-        read_product(3, 0)
-        update_add(2, 0)
-        read_product(3, 1)
-        update_add(2, 1)
-        read_square(3, 0)
-        decay_product(4, 0)
-        query_quantize(5)
-        read_square(3, 1)
-        decay_product(4, 1)
+        query_quantize(3)
         quantize_rows(19)
-        update_product(3, 0)
-        query_scale(6)
-        decay_scale(4, 0)
+        update_start(1, 1)
+        read_square(2, 1)
+        update_add(1, 1, 0)
+        update_add(1, 1, 1)
+        query_exp(5, 1)
+        read_norm(2)
+        update_add(1, 1, 2)
+        update_start(2, 0)
+        query_exp(5, 0)
+        update_add(2, 0, 0)
+        read_out(2, 1)
+        update_add(2, 0, 1)
+        update_out(1, 1)
+        update_add(2, 0, 2)
+        read_out(2, 0)
+        read_product(3, 0)
+        query_exp(4, 0)
+        read_product(3, 1)
+        update_out(2, 0)
+        query_scale(4)
+        update_start(2, 1)
+        read_square(3, 0)
+        update_add(2, 1, 0)
+        update_add(2, 1, 1)
+        read_square(3, 1)
+        query_scale(5)
+        update_add(2, 1, 2)
+        update_start(3, 0)
         read_norm(3)
-        decay_scale(4, 1)
-        query_product(7)
-        update_add(3, 0)
-        update_product(3, 1)
-        query_exp(7, 1)
-        read_out(3, 1)
-        query_exp(7, 0)
-        decay_product(5, 0)
+        update_out(2, 1)
+        update_add(3, 0, 0)
+        update_add(3, 0, 1)
+        query_quantize(4)
+        update_add(3, 0, 2)
+        query_quantize(5)
+        query_product(6)
         read_out(3, 0)
+        update_out(3, 0)
+        update_start(3, 1)
+        read_out(3, 1)
+        update_add(3, 1, 0)
+        query_exp(6, 1)
         read_product(4, 0)
-        decay_scale(5, 0)
-        update_add(3, 1)
+        query_exp(6, 0)
         read_product(4, 1)
         read_square(4, 0)
-        query_scale(7)
-        decay_product(5, 1)
+        query_scale(6)
+        update_add(3, 1, 1)
+        update_add(3, 1, 2)
         read_square(4, 1)
-        update_product(4, 0)
-        decay_scale(5, 1)
+        query_product(7)
+        update_out(3, 1)
         read_norm(4)
         query_quantize(6)
-        update_product(4, 1)
-        update_add(4, 0)
-        read_out(4, 1)
-        decay_product(6, 0)
-        decay_product(6, 1)
-        decay_scale(6, 0)
+        update_start(4, 0)
+        query_exp(7, 0)
+        update_add(4, 0, 0)
         read_out(4, 0)
+        update_add(4, 0, 1)
+        query_exp(7, 1)
+        update_add(4, 0, 2)
+        read_out(4, 1)
         read_product(5, 0)
-        update_add(4, 1)
+        update_out(4, 0)
+        query_scale(7)
         read_product(5, 1)
         read_square(5, 0)
-        update_product(5, 0)
-        query_quantize(7)
+        update_start(4, 1)
         read_square(5, 1)
-        decay_scale(6, 1)
-        update_product(5, 1)
+        update_add(4, 1, 0)
+        update_add(4, 1, 1)
+        query_quantize(7)
+        update_add(4, 1, 2)
         read_norm(5)
-        update_add(5, 0)
-        decay_product(7, 0)
+        update_start(5, 0)
+        update_out(4, 1)
+        update_add(5, 0, 0)
         read_out(5, 0)
-        decay_product(7, 1)
-        decay_scale(7, 0)
+        update_add(5, 0, 1)
+        update_add(5, 0, 2)
         read_out(5, 1)
         read_product(6, 0)
-        update_add(5, 1)
+        update_out(5, 0)
         read_product(6, 1)
         read_square(6, 0)
-        update_product(6, 0)
+        update_start(5, 1)
         read_square(6, 1)
-        decay_scale(7, 1)
-        update_product(6, 1)
+        update_add(5, 1, 0)
+        update_add(5, 1, 1)
+        update_add(5, 1, 2)
         read_norm(6)
-        update_add(6, 0)
-        update_product(7, 0)
-        read_out(6, 0)
-        update_add(6, 1)
-        update_product(7, 1)
+        update_start(6, 0)
+        update_out(5, 1)
+        update_add(6, 0, 0)
         read_out(6, 1)
+        update_add(6, 0, 1)
+        update_add(6, 0, 2)
+        read_out(6, 0)
         read_product(7, 0)
+        update_out(6, 0)
         read_product(7, 1)
-        update_add(7, 1)
         read_square(7, 0)
-        update_add(7, 0)
+        update_start(6, 1)
         read_square(7, 1)
+        update_add(6, 1, 0)
+        update_add(6, 1, 1)
+        update_add(6, 1, 2)
         read_norm(7)
+        update_start(7, 0)
+        update_out(6, 1)
+        update_add(7, 0, 0)
         read_out(7, 1)
+        update_add(7, 0, 1)
+        update_add(7, 0, 2)
         read_out(7, 0)
+        update_start(7, 1)
+        update_out(7, 0)
+        update_add(7, 1, 0)
+        update_add(7, 1, 1)
+        update_add(7, 1, 2)
+        update_out(7, 1)

@@ -19,12 +19,16 @@ M, T, K, R, F, D = 1024, 1536, 1024, 512, 1024, 1024
 EPS = 1e-6
 FLOPS = 2 * (M * K * R + T * K * R + M * F * D + T * F * D)
 
-TPB, ABB, CB, SDB = 1,2,2,3
-UPDATE_ON_VECTOR = ()
+TPB, ABB, CB, SDB = 1,1,4,2
+KEY_TURNS = 12
+UPDATE_ON_VECTOR = ((3, 0), (4, 1), (6, 1), (7, 0))
+COPY_ON_VECTOR = (3,)
+WIDEN_ON_VECTOR = (2, 3, 5, 7, 10, 11)
+SINGLES = 2
+XTB = 2
 KG = K // 512
 TG = T // 512
 FG = F // 512
-WIDEN_ON_VECTOR = (0, 1, 2, 3, 7, 11)
 
 
 def tile_performer_state_step_f7_kernel(
@@ -66,11 +70,21 @@ def tile_performer_state_step_f7_kernel(
         sds = cst.tile([P, FG, 2, D], U8, name="sds", align_bytes=64)
         gn = cst.tile([P, D], BF16, name="gn")
 
-        nc.gpsimd.memset(osc[:].bitcast(I32), 0)
+        quarter = cst.tile([P, TG * 4], F32, name="quarter")
+        mhalf = cst.tile([P, 1], F32, name="mhalf")
+        mask = cst.tile([P, 8], I32, name="mask")
+        one = cst.tile([P, 1], F32, name="one")
+        dk = cst.tile([P, 4, 32, 16], BF16, name="dk", align_bytes=64)
+        dz = cst.tile([P, 2, 4 * P], U32, name="dz", align_bytes=64)
+        nc.vector.memset(osc[:].bitcast(I32), 0)
+        nc.vector.memset(one[:], 1.0)
+        nc.vector.memset(quarter[:], 0.25)
+        nc.vector.memset(mhalf[:], -0.5)
+        nc.vector.memset(mask[:], -983056)
         identf = cst.tile([P, P], F32, name="identf")
         make_identity(nc, identf[:])
-        nc.gpsimd.memset(ssc[:].bitcast(I32), 0)
-        nc.gpsimd.memset(sds[:].rearrange("p s j n -> p (s j n)").bitcast(I32), 0)
+        nc.vector.memset(ssc[:].bitcast(I32), 0)
+        nc.vector.memset(sds[:].rearrange("p s j n -> p (s j n)").bitcast(I32), 0)
 
         vview = values_bytes.rearrange("(g p t) d -> g p t d", p=P, t=4)
         oview = omega_scales.rearrange("g (q r) n -> r q g n", r=4)
@@ -115,20 +129,17 @@ def tile_performer_state_step_f7_kernel(
             )
         nc.sync.dma_start(out=gn[:], in_=gain.partition_broadcast(P))
 
-        quarter = cst.tile([P, TG * 4], F32, name="quarter")
-        nc.vector.memset(quarter[:], 0.25)
-        mhalf = cst.tile([P, 1], F32, name="mhalf")
-        nc.vector.memset(mhalf[:], -0.5)
         kbias = cst.tile([P, TG * 4], F32, name="kbias")
         vss = cst.tile([P, TG * 4], F32, name="vss")
 
         klow = cst.tile([P, 2, 2, 4], BF16, name="klow")
-        mask = cst.tile([P, 8], I32, name="mask")
         eye = cst.tile([P, 32], BF16, name="eye")
-        dk = cst.tile([P, 4, 32, 16], BF16, name="dk", align_bytes=64)
         dcod = cst.tile([P, 4 * P], U32, name="dcod", align_bytes=64)
         dsc = cst.tile([P, 4 * P], U8, name="dsc", align_bytes=64)
-        dz = cst.tile([P, 2, 4 * P], U32, name="dz", align_bytes=64)
+        spare = cst.tile([P, 1], F32, name="spare")
+        nc.scalar.activation(out=spare[:], in_=one[:], func=ACTF.Ln)
+        nc.vector.memset(dz[:].bitcast(I32), 0)
+        nc.vector.memset(dk[:].rearrange("p c r x -> p (c r x)").bitcast(F32), 0.0)
 
         owp = cst.tile([P, KG, 4, P, 2], U8, name="owp", align_bytes=64)
         osp = cst.tile([P, KG, 4, P], U8, name="osp", align_bytes=64)
@@ -149,7 +160,8 @@ def tile_performer_state_step_f7_kernel(
 
         def transposes(i):
             words = rows(i)[:].bitcast(F32)
-            tp = ps.tile([P, KG, 2, P], F32, name="tp", bufs=TPB)
+            early = i < KEY_TURNS
+            tp = ps.tile([P, KG, 2, P], F32, name="tp", tag="cb" if early else "tp", bufs=CB if early else TPB)
             for g in range(KG):
                 for u in range(2):
                     nc.tensor.transpose(
@@ -157,19 +169,34 @@ def tile_performer_state_step_f7_kernel(
                     )
             st["tp", i] = tp
 
-        def copy_out(i):
-            xt = wk.tile([P, KG * P * 4], BF16, name="xt", align_bytes=64)
-            nc.scalar.copy(
-                out=xt[:].bitcast(F32).rearrange("p (g r u) -> p g r u", g=KG, u=2),
-                in_=st["tp", i][:].rearrange("p g u r -> p g r u"),
-            )
-            st["xt", i] = xt
+        def pair(i):
+            if i < SINGLES:
+                return i, 0
+            return SINGLES + (i - SINGLES) // 2, (i - SINGLES) % 2
 
-        def quantize_rows(i):
-            xq = wk.tile([P, KG * P], U32, name="xq", align_bytes=64)
-            xs = wk.tile([P, KG * P], U8, name="xs", align_bytes=64)
-            nc.vector.quantize_mx(out=xq[:].bitcast(FP8X4), scales=xs[:], in_=st["xt", i][:])
-            st["xq", i] = (xq, xs)
+        def copy_out(i):
+            j, n = pair(i)
+            if ("xt", j) not in st:
+                xt = wk.tile([P, 2 * KG * P * 4], BF16, name="xt", bufs=XTB, align_bytes=64)
+                st["xt", j] = xt
+            dst = st["xt", j][:, 1024 * n : 1024 * (n + 1)].bitcast(F32).rearrange("p (g r u) -> p g r u", g=KG, u=2)
+            src = st["tp", i][:].rearrange("p g u r -> p g r u")
+            if i in COPY_ON_VECTOR:
+                nc.vector.tensor_copy(out=dst, in_=src)
+            else:
+                nc.scalar.copy(out=dst, in_=src)
+
+        def quantize_rows(j):
+            n = 1 if j < SINGLES else 2
+            xq = wk.tile([P, 2 * KG * P], U32, name="xq", bufs=3, align_bytes=64)
+            xs = wk.tile([P, 2 * KG * P], U8, name="xs", bufs=3, align_bytes=64)
+            nc.vector.quantize_mx(
+                out=xq[:, 0 : 256 * n].bitcast(FP8X4), scales=xs[:, 0 : 256 * n],
+                in_=st["xt", j][:, 0 : 1024 * n],
+            )
+            for k in range(n):
+                i = j if n == 1 else SINGLES + 2 * (j - SINGLES) + k
+                st["xq", i] = (xq[:, 256 * k : 256 * (k + 1)], xs[:, 256 * k : 256 * (k + 1)])
 
         def widen(i):
             g, t = divmod(i, 4)
@@ -191,12 +218,10 @@ def tile_performer_state_step_f7_kernel(
                 in_=planes.rearrange("p t (c i) -> p c t i", i=4),
             )
 
-        def values_interleave(g, h):
-            if ("vint", g) not in st:
-                vint = wk.tile([P, D * 4], BF16, name="vint", bufs=2, align_bytes=64)
-                st["vint", g] = vint
-            half = slice(512 * h, 512 * (h + 1))
-            interleave(st["vint", g][:, 2048 * h : 2048 * (h + 1)], st["vpl", g][:, :, half])
+        def values_interleave(g):
+            vint = wk.tile([P, D * 4], BF16, name="vint", bufs=1, align_bytes=64)
+            interleave(vint[:], st["vpl", g][:])
+            st["vint", g] = vint
 
         def values_quantize(g):
             nc.vector.quantize_mx(
@@ -294,7 +319,7 @@ def tile_performer_state_step_f7_kernel(
 
         def read_product(m, h):
             pqq, pqs = st["pqq", m]
-            cb = ps.tile([P, 512], F32, name="cb", bufs=CB)
+            cb = ps.tile([P, 512], F32, name="cb", tag="cb", bufs=CB)
             for s in range(2):
                 nc.tensor.matmul_mx(
                     out=cb[:],
@@ -330,7 +355,7 @@ def tile_performer_state_step_f7_kernel(
         def read_out(m, h):
             last = ("yt", m) in st
             if not last:
-                yt = wk.tile([P, D], F32, name="yt", bufs=2)
+                yt = wk.tile([P, D], F32, name="yt", bufs=3)
                 st["yt", m] = yt
             yt = st["yt", m]
             nc.vector.scalar_tensor_tensor(
@@ -338,18 +363,17 @@ def tile_performer_state_step_f7_kernel(
                 scalar=st["rstd", m][:], in1=gn[:, 512 * h : 512 * (h + 1)],
                 op0=ALU.mult, op1=ALU.mult,
             )
-            if last:
+            if m == 7:
+                nc.sync.dma_start(
+                    out=out_0[P * m : P * (m + 1), 512 * h : 512 * (h + 1)], in_=yt[:, 512 * h : 512 * (h + 1)]
+                )
+            elif last:
                 nc.sync.dma_start(out=out_0[P * m : P * (m + 1), :], in_=yt[:])
 
         def decay_eye():
             half = wk.tile([P, 64], F32, name="half", bufs=1)
             nc.gpsimd.tensor_tensor(out=half[:], in0=identf[:, 0:64], in1=identf[:, 64:128], op=ALU.add)
             nc.gpsimd.tensor_tensor(out=eye[:], in0=half[:, 0:32], in1=half[:, 32:64], op=ALU.add)
-
-        def decay_zero():
-            nc.gpsimd.memset(dz[:].bitcast(I32), 0)
-            nc.gpsimd.memset(dk[:].rearrange("p c r x -> p (c r x)"), 0.0)
-            nc.gpsimd.memset(mask[:], -983056)
 
         def decay_split():
             flat = kk[:].rearrange("p s j t -> p (s j t)")
@@ -423,7 +447,11 @@ def tile_performer_state_step_f7_kernel(
                 nc.vector.tensor_copy(out=nt[:, 512 * h : 512 * (h + 1)], in_=st["d", n, h][:])
             else:
                 nc.scalar.copy(out=nt[:, 512 * h : 512 * (h + 1)], in_=st["d", n, h][:])
-            if last:
+            if n == 7:
+                nc.sync.dma_start(
+                    out=out_1[P * n : P * (n + 1), 512 * h : 512 * (h + 1)], in_=nt[:, 512 * h : 512 * (h + 1)]
+                )
+            elif last:
                 nc.sync.dma_start(out=out_1[P * n : P * (n + 1), :], in_=nt[:])
 
         def sign_and_scale():
@@ -458,6 +486,7 @@ def tile_performer_state_step_f7_kernel(
         def write_ln():
             wln = cst.tile([P, TG * 4], F32, name="wln")
             nc.scalar.activation(out=wln[:], in_=st["wclip"][:], func=ACTF.Ln)
+            nc.scalar.activation(out=spare[:], in_=one[:], func=ACTF.Exp)
             st["wln"] = wln
 
         def write_bias():
@@ -467,323 +496,310 @@ def tile_performer_state_step_f7_kernel(
             )
 
 
-        decay_zero()
         transposes(0)
-        sign_and_scale()
-        decay_eye()
         write_abs()
-        copy_out(0)
-        write_clip()
-        write_ln()
-        quantize_rows(0)
         transposes(1)
-        widen(2)
+        copy_out(0)
         copy_out(1)
+        sign_and_scale()
+        write_clip()
+        quantize_rows(0)
         widen(3)
-        widen(1)
-        transposes(2)
-        write_bias()
         quantize_rows(1)
-        copy_out(2)
-        widen(0)
-        transposes(3)
-        quantize_rows(2)
-        widen(4)
-        values_interleave(0, 0)
-        copy_out(3)
-        key_product(0)
-        permute_scales(1)
-        widen(5)
-        key_product(1)
-        permute_scales(0)
-        transposes(4)
-        decay_split()
-        quantize_rows(3)
-        key_exp(1, 1)
-        values_interleave(0, 1)
-        key_exp(0, 0)
-        key_exp(1, 0)
+        transposes(2)
         permute_omega(1)
-        key_exp(0, 1)
-        key_product(2)
-        widen(9)
-        key_product(3)
-        values_quantize(0)
-        key_exp(3, 0)
-        widen(7)
-        key_exp(2, 0)
+        widen(1)
+        write_ln()
+        key_product(1)
+        transposes(3)
+        write_bias()
+        key_exp(1, 0)
+        key_exp(1, 1)
+        copy_out(2)
+        permute_scales(0)
         permute_omega(0)
-        key_exp(2, 1)
-        key_exp(3, 1)
-        features_interleave(0, 0)
-        widen(8)
-        features_interleave(0, 1)
-        copy_out(4)
-        widen(6)
-        transposes(5)
-        quantize_rows(4)
-        features_quantize(0, 0)
-        copy_out(5)
-        key_product(4)
-        values_interleave(1, 0)
-        widen(10)
+        widen(2)
+        copy_out(3)
+        widen(0)
+        key_product(0)
         transposes(6)
-        key_exp(4, 1)
-        quantize_rows(5)
-        values_interleave(1, 1)
-        key_exp(4, 0)
-        key_product(5)
-        copy_out(6)
-        key_exp(5, 0)
-        widen(11)
+        widen(5)
+        quantize_rows(2)
         transposes(7)
-        quantize_rows(6)
-        key_exp(5, 1)
-        values_interleave(2, 0)
-        key_product(6)
+        key_exp(0, 1)
+        key_exp(0, 0)
+        transposes(5)
+        transposes(4)
+        copy_out(6)
+        decay_split()
         copy_out(7)
-        key_exp(6, 1)
-        transposes(8)
-        quantize_rows(7)
-        features_quantize(0, 1)
-        key_exp(6, 0)
+        key_product(2)
+        values_interleave(0)
+        key_exp(2, 0)
+        quantize_rows(4)
+        key_exp(2, 1)
+        copy_out(5)
+        key_product(3)
+        widen(7)
+        copy_out(4)
+        key_exp(3, 1)
+        widen(11)
+        permute_scales(1)
+        decay_eye()
+        key_exp(3, 0)
         key_product(7)
-        values_quantize(1)
-        copy_out(8)
-        key_exp(7, 0)
-        transposes(9)
-        key_exp(7, 1)
-        quantize_rows(8)
-        features_interleave(1, 0)
-        copy_out(9)
-        key_product(8)
-        key_exp(8, 1)
         transposes(10)
-        quantize_rows(9)
-        features_interleave(1, 1)
-        key_exp(8, 0)
-        key_product(9)
-        copy_out(10)
-        key_exp(9, 1)
-        quantize_rows(10)
         transposes(11)
-        values_interleave(2, 1)
-        key_exp(9, 0)
-        key_product(10)
+        widen(4)
+        key_exp(7, 0)
+        quantize_rows(3)
+        features_interleave(0, 1)
+        key_exp(7, 1)
         copy_out(11)
-        key_exp(10, 1)
-        quantize_rows(11)
+        copy_out(10)
+        features_interleave(0, 0)
         transposes(12)
-        values_quantize(2)
-        key_exp(10, 0)
-        key_product(11)
         copy_out(12)
         decay_build()
-        key_exp(11, 1)
-        quantize_rows(12)
-        transposes(13)
+        features_quantize(0, 1)
+        transposes(8)
         decay_quantize()
-        key_exp(11, 0)
-        query_product(0)
-        features_quantize(1, 1)
+        key_product(6)
+        transposes(13)
+        key_exp(6, 0)
+        key_exp(6, 1)
+        transposes(9)
+        values_quantize(0)
+        widen(6)
+        key_product(4)
         copy_out(13)
-        decay_place()
-        query_exp(0, 0)
+        quantize_rows(6)
+        key_exp(4, 0)
+        key_exp(4, 1)
         transposes(14)
-        quantize_rows(13)
-        query_exp(0, 1)
-        features_interleave(2, 0)
-        query_product(1)
+        quantize_rows(7)
+        key_product(5)
+        copy_out(9)
+        decay_place()
+        widen(10)
         copy_out(14)
-        update_start(0, 0)
-        query_exp(1, 0)
+        key_exp(5, 1)
+        key_exp(5, 0)
+        widen(8)
+        values_interleave(1)
+        query_product(0)
+        query_exp(0, 0)
+        query_exp(0, 1)
+        key_product(10)
+        features_quantize(0, 0)
+        values_quantize(1)
+        widen(9)
+        key_exp(10, 0)
+        key_exp(10, 1)
         transposes(15)
-        query_scale(0)
-        query_exp(1, 1)
-        update_add(0, 0, 0)
+        update_start(0, 0)
+        key_product(11)
+        copy_out(8)
         copy_out(15)
-        update_start(0, 1)
-        update_add(0, 1, 0)
-        query_scale(1)
-        update_start(1, 0)
+        features_interleave(1, 0)
+        query_scale(0)
         transposes(16)
-        query_quantize(0)
-        update_add(1, 0, 0)
+        key_exp(11, 1)
+        quantize_rows(5)
+        key_exp(11, 0)
+        update_start(0, 1)
         copy_out(16)
-        query_quantize(1)
-        read_product(0, 0)
-        quantize_rows(14)
-        quantize_rows(15)
-        read_product(0, 1)
-        features_quantize(1, 0)
-        read_square(0, 0)
+        key_product(9)
+        key_exp(9, 0)
         transposes(17)
-        features_quantize(2, 0)
-        read_square(0, 1)
-        query_product(2)
-        features_interleave(2, 1)
+        update_add(0, 0, 0)
+        features_quantize(1, 0)
+        key_exp(9, 1)
+        query_quantize(0)
         copy_out(17)
-        read_norm(0)
-        update_add(1, 0, 1)
-        query_exp(2, 0)
-        update_add(0, 1, 1)
-        update_add(0, 1, 2)
-        read_out(0, 1)
-        query_exp(2, 1)
+        read_product(0, 1)
+        values_interleave(2)
+        key_product(8)
+        read_square(0, 1)
+        update_add(0, 1, 0)
+        quantize_rows(8)
         transposes(18)
-        read_out(0, 0)
-        update_out(0, 1)
-        read_product(1, 0)
-        features_quantize(2, 1)
+        values_quantize(2)
+        read_product(0, 0)
+        key_exp(8, 0)
+        key_exp(8, 1)
+        update_add(0, 1, 1)
         copy_out(18)
-        read_product(1, 1)
-        read_square(1, 0)
-        query_scale(2)
-        update_add(0, 0, 1)
-        read_square(1, 1)
-        update_add(0, 0, 2)
-        query_product(3)
-        quantize_rows(16)
-        update_out(0, 0)
-        read_norm(1)
-        query_quantize(2)
+        query_product(2)
+        read_square(0, 0)
+        query_exp(2, 1)
+        features_interleave(2, 0)
+        features_quantize(2, 0)
         transposes(19)
-        query_exp(3, 1)
-        quantize_rows(17)
-        read_out(1, 1)
-        update_add(1, 0, 2)
-        query_exp(3, 0)
-        query_product(4)
-        read_out(1, 0)
-        update_out(1, 0)
-        query_scale(3)
-        read_product(2, 0)
+        update_add(0, 0, 1)
+        query_exp(2, 0)
         copy_out(19)
-        read_product(2, 1)
-        query_exp(4, 1)
-        quantize_rows(18)
-        query_product(5)
-        read_square(2, 0)
-        query_quantize(3)
-        quantize_rows(19)
-        update_start(1, 1)
-        read_square(2, 1)
-        update_add(1, 1, 0)
-        update_add(1, 1, 1)
-        query_exp(5, 1)
-        read_norm(2)
-        update_add(1, 1, 2)
+        update_add(0, 0, 2)
+        update_out(0, 0)
+        query_product(1)
+        update_add(0, 1, 2)
+        features_interleave(1, 1)
         update_start(2, 0)
-        query_exp(5, 0)
         update_add(2, 0, 0)
-        read_out(2, 1)
+        update_out(0, 1)
+        query_exp(1, 1)
         update_add(2, 0, 1)
-        update_out(1, 1)
+        query_scale(2)
+        query_exp(1, 0)
+        quantize_rows(10)
         update_add(2, 0, 2)
-        read_out(2, 0)
-        read_product(3, 0)
-        query_exp(4, 0)
-        read_product(3, 1)
-        update_out(2, 0)
-        query_scale(4)
+        read_norm(0)
         update_start(2, 1)
-        read_square(3, 0)
+        update_out(2, 0)
         update_add(2, 1, 0)
+        query_quantize(2)
         update_add(2, 1, 1)
-        read_square(3, 1)
-        query_scale(5)
         update_add(2, 1, 2)
-        update_start(3, 0)
-        read_norm(3)
         update_out(2, 1)
+        query_product(3)
+        read_product(2, 0)
+        read_out(0, 0)
+        update_start(1, 0)
+        quantize_rows(9)
+        update_add(1, 0, 0)
+        query_scale(1)
+        update_add(1, 0, 1)
+        query_exp(3, 0)
+        read_out(0, 1)
+        query_exp(3, 1)
+        update_start(3, 0)
+        update_add(1, 0, 2)
         update_add(3, 0, 0)
+        read_product(2, 1)
         update_add(3, 0, 1)
-        query_quantize(4)
+        read_square(2, 0)
+        query_quantize(1)
+        update_out(1, 0)
+        query_product(4)
+        update_start(1, 1)
         update_add(3, 0, 2)
-        query_quantize(5)
-        query_product(6)
-        read_out(3, 0)
+        update_add(1, 1, 0)
+        read_square(2, 1)
+        query_exp(4, 1)
+        features_quantize(1, 1)
+        read_norm(2)
+        update_add(1, 1, 1)
+        query_exp(4, 0)
+        query_scale(3)
+        features_interleave(2, 1)
+        update_add(1, 1, 2)
+        read_product(1, 0)
         update_out(3, 0)
+        read_product(1, 1)
+        query_product(5)
         update_start(3, 1)
-        read_out(3, 1)
+        update_out(1, 1)
+        read_square(1, 0)
+        read_square(1, 1)
+        query_quantize(3)
+        read_out(2, 0)
         update_add(3, 1, 0)
-        query_exp(6, 1)
-        read_product(4, 0)
-        query_exp(6, 0)
-        read_product(4, 1)
-        read_square(4, 0)
-        query_scale(6)
+        query_exp(5, 0)
         update_add(3, 1, 1)
         update_add(3, 1, 2)
-        read_square(4, 1)
-        query_product(7)
+        read_out(2, 1)
+        query_exp(5, 1)
         update_out(3, 1)
-        read_norm(4)
-        query_quantize(6)
+        read_product(3, 1)
+        read_square(3, 1)
+        query_scale(4)
+        read_norm(1)
+        features_quantize(2, 1)
         update_start(4, 0)
-        query_exp(7, 0)
-        update_add(4, 0, 0)
-        read_out(4, 0)
-        update_add(4, 0, 1)
-        query_exp(7, 1)
-        update_add(4, 0, 2)
-        read_out(4, 1)
-        read_product(5, 0)
-        update_out(4, 0)
-        query_scale(7)
-        read_product(5, 1)
-        read_square(5, 0)
-        update_start(4, 1)
-        read_square(5, 1)
-        update_add(4, 1, 0)
-        update_add(4, 1, 1)
-        query_quantize(7)
-        update_add(4, 1, 2)
-        read_norm(5)
+        read_product(3, 0)
+        query_product(6)
         update_start(5, 0)
-        update_out(4, 1)
+        update_add(4, 0, 0)
+        query_quantize(4)
+        read_square(3, 0)
+        query_exp(6, 1)
+        query_exp(6, 0)
+        update_add(4, 0, 1)
         update_add(5, 0, 0)
-        read_out(5, 0)
+        read_out(1, 0)
+        update_add(4, 0, 2)
+        read_product(4, 0)
+        read_norm(3)
+        read_out(1, 1)
+        read_product(4, 1)
+        update_out(4, 0)
+        query_product(7)
+        read_square(4, 0)
         update_add(5, 0, 1)
+        update_start(4, 1)
+        update_add(4, 1, 0)
+        query_scale(5)
+        read_out(3, 0)
+        read_square(4, 1)
+        read_norm(4)
+        query_exp(7, 0)
         update_add(5, 0, 2)
-        read_out(5, 1)
-        read_product(6, 0)
+        query_quantize(5)
+        update_add(4, 1, 1)
+        query_exp(7, 1)
         update_out(5, 0)
-        read_product(6, 1)
-        read_square(6, 0)
+        read_out(3, 1)
+        update_add(4, 1, 2)
+        query_scale(6)
+        read_product(5, 0)
+        read_square(5, 0)
+        read_product(5, 1)
+        update_out(4, 1)
+        read_out(4, 0)
         update_start(5, 1)
-        read_square(6, 1)
+        read_square(5, 1)
         update_add(5, 1, 0)
         update_add(5, 1, 1)
-        update_add(5, 1, 2)
-        read_norm(6)
+        query_quantize(6)
         update_start(6, 0)
-        update_out(5, 1)
+        update_add(5, 1, 2)
+        read_product(6, 0)
+        read_out(4, 1)
+        read_product(6, 1)
         update_add(6, 0, 0)
-        read_out(6, 1)
+        update_out(5, 1)
+        update_start(6, 1)
+        update_add(6, 1, 0)
         update_add(6, 0, 1)
         update_add(6, 0, 2)
-        read_out(6, 0)
-        read_product(7, 0)
+        read_norm(5)
+        read_square(6, 0)
+        query_scale(7)
+        read_square(6, 1)
         update_out(6, 0)
-        read_product(7, 1)
-        read_square(7, 0)
-        update_start(6, 1)
-        read_square(7, 1)
-        update_add(6, 1, 0)
         update_add(6, 1, 1)
         update_add(6, 1, 2)
-        read_norm(7)
-        update_start(7, 0)
+        read_out(5, 0)
+        query_quantize(7)
+        read_out(5, 1)
+        read_product(7, 0)
         update_out(6, 1)
+        read_product(7, 1)
+        read_norm(6)
+        update_start(7, 0)
+        read_square(7, 0)
         update_add(7, 0, 0)
-        read_out(7, 1)
         update_add(7, 0, 1)
+        read_square(7, 1)
         update_add(7, 0, 2)
-        read_out(7, 0)
+        read_out(6, 0)
         update_start(7, 1)
-        update_out(7, 0)
         update_add(7, 1, 0)
+        read_norm(7)
         update_add(7, 1, 1)
+        read_out(6, 1)
+        update_out(7, 0)
         update_add(7, 1, 2)
         update_out(7, 1)
+        read_out(7, 1)
+        read_out(7, 0)

@@ -20,12 +20,18 @@ EPS = 1e-6
 FLOPS = 2 * (M * K * R + T * K * R + M * F * D + T * F * D)
 
 TPB, ABB, CB, SDB = 1,1,4,2
-KEY_TURNS = 12
-UPDATE_ON_VECTOR = ((3, 0), (4, 1), (6, 1), (7, 0))
-COPY_ON_VECTOR = (3,)
-WIDEN_ON_VECTOR = (2, 3, 5, 7, 10, 11)
+KEY_TURNS = 8
+EARLY = (0, 1, 2, 3)
+UPDATE_ON_VECTOR = ((0, 0), (1, 0), (6, 1))
+PART_ON_VECTOR = ()
+COPY_ON_VECTOR = (1,)
+WIDEN_ON_VECTOR = (1, 2, 3, 6, 8, 11)
 SINGLES = 2
 XTB = 2
+ROWB = 14
+MERGED = 2
+QPAIRS = 0
+PARTIAL = 0
 KG = K // 512
 TG = T // 512
 FG = F // 512
@@ -46,12 +52,9 @@ def tile_performer_state_step_f7_kernel(
         kview = keys.rearrange("(g p t) k -> g t p k", p=P, t=4)
         kraw = []
         for i in range(12):
-            kr = raw.tile([P, K], BF16, name=f"kraw{i}", align_bytes=64)
+            kr = raw.tile([P, K], BF16, name="rows", bufs=ROWB, align_bytes=64)
             kraw.append(kr)
         qraw = []
-        for m in range(8):
-            qr = raw.tile([P, K], BF16, name=f"qraw{m}", align_bytes=64)
-            qraw.append(qr)
         vbytes = []
         for g in range(TG):
             vb = raw.tile([P, 4, D], U8, name=f"vbytes{g}", align_bytes=64)
@@ -113,8 +116,10 @@ def tile_performer_state_step_f7_kernel(
         nc.sync.dma_start(out=sw[:], in_=state_words.rearrange("g p n t -> p g (n t)"))
         for r in range(4):
             nc.sync.dma_start(out=ssc[r:P:32, :, :].bitcast(I32), in_=sview[r].bitcast(I32))
-        for m in range(8):
-            nc.sync.dma_start(out=qraw[m][:], in_=queries[P * m : P * (m + 1), :])
+        for m in range(ROWB - 12):
+            qr = raw.tile([P, K], BF16, name="rows", bufs=ROWB, align_bytes=64)
+            qraw.append(qr)
+            nc.sync.dma_start(out=qr[:], in_=queries[P * m : P * (m + 1), :])
         wview = state_words.rearrange("s (j b r) n t -> s j b r (n t)", j=2, b=2)
         for s in range(FG):
             for j in range(2):
@@ -154,6 +159,11 @@ def tile_performer_state_step_f7_kernel(
             vq.append(c)
             vsc.append(d)
         st = {}
+
+        def load_rows(m):
+            qr = raw.tile([P, K], BF16, name="rows", bufs=ROWB, align_bytes=64)
+            qraw.append(qr)
+            nc.sync.dma_start(out=qr[:], in_=queries[P * m : P * (m + 1), :])
 
         def rows(i):
             return kraw[i] if i < 12 else qraw[i - 12]
@@ -219,7 +229,7 @@ def tile_performer_state_step_f7_kernel(
             )
 
         def values_interleave(g):
-            vint = wk.tile([P, D * 4], BF16, name="vint", bufs=1, align_bytes=64)
+            vint = wk.tile([P, D * 4], BF16, name="inter", bufs=2, align_bytes=64)
             interleave(vint[:], st["vpl", g][:])
             st["vint", g] = vint
 
@@ -246,23 +256,24 @@ def tile_performer_state_step_f7_kernel(
         def key_exp(i, s):
             g, t = divmod(i, 4)
             if ("pl", g) not in st:
-                pl = wk.tile([P, 2, 4, R], BF16, name="pl", bufs=2, align_bytes=64)
+                pl = wk.tile([P, 4, 2 * R], BF16, name="pl", bufs=2, align_bytes=64)
                 st["pl", g] = pl
             nc.scalar.activation(
-                out=st["pl", g][:, s, t, :], in_=st["b", i][:], func=ACTF.Exp,
+                out=st["pl", g][:, t, R * s : R * (s + 1)], in_=st["b", i][:], func=ACTF.Exp,
                 bias=kbias[:, i : i + 1], scale=1.0 - 2.0 * s,
             )
 
         def features_interleave(g, s):
-            pint = wk.tile([P, R * 4], BF16, name="pint", bufs=2, align_bytes=64)
-            interleave(pint[:], st["pl", g][:, s])
-            st["pint", g, s] = pint
+            cols = slice(0, 2 * R) if g < MERGED else slice(R * s, R * (s + 1))
+            pint = wk.tile([P, 2 * R * 4], BF16, name="inter", bufs=2, align_bytes=64)
+            pint = pint[:, 0 : 4 * (cols.stop - cols.start)]
+            interleave(pint, st["pl", g][:, :, cols])
+            st["pint", g, s] = pint, cols
 
         def features_quantize(g, s):
+            pint, cols = st["pint", g, s]
             nc.vector.quantize_mx(
-                out=pkq[g][:, R * s : R * (s + 1)].bitcast(FP8X4),
-                scales=pks[g][:, R * s : R * (s + 1)],
-                in_=st["pint", g, s][:],
+                out=pkq[g][:, cols].bitcast(FP8X4), scales=pks[g][:, cols], in_=pint
             )
 
         def permute_omega(c):
@@ -291,40 +302,50 @@ def tile_performer_state_step_f7_kernel(
                     )
             st["a", m] = bank
 
+        def qpair(m):
+            if m < 2 * QPAIRS:
+                return m // 2, m % 2, 2
+            return m - QPAIRS, 0, 1
+
         def query_exp(m, s):
-            if ("ex", m) not in st:
-                ex = wk.tile([P, 2, P, 4], F32, name="ex", bufs=2)
-                st["ex", m] = ex
+            j, k, n = qpair(m)
+            if ("ex", j) not in st:
+                ex = wk.tile([P, 2, n, P, 4], F32, name="ex", bufs=2)
+                st["ex", j] = ex
             nc.scalar.activation(
-                out=st["ex", m][:, s], in_=st["a", m][:].rearrange("p t n -> p n t"), func=ACTF.Exp,
+                out=st["ex", j][:, s, k], in_=st["a", m][:].rearrange("p t n -> p n t"), func=ACTF.Exp,
                 scale=1.0 - 2.0 * s,
             )
 
-        def query_scale(m):
-            pq = wk.tile([P, 2, P, 4], BF16, name="pq", bufs=2, align_bytes=64)
+        def query_scale(j):
+            n = 2 if j < QPAIRS else 1
+            pq = wk.tile([P, 2, n * P, 4], BF16, name="pq", bufs=2, align_bytes=64)
             nc.vector.tensor_tensor(
-                out=pq[:], in0=st["ex", m][:],
-                in1=rd[:].unsqueeze(2).to_broadcast([P, 2, P, 4]), op=ALU.mult,
+                out=pq[:], in0=st["ex", j][:].rearrange("p s k n t -> p s (k n) t"),
+                in1=rd[:].unsqueeze(2).to_broadcast([P, 2, n * P, 4]), op=ALU.mult,
             )
-            st["pq", m] = pq
+            st["pq", j] = pq
 
-        def query_quantize(m):
-            pqq = wk.tile([P, 2 * P], U32, name="pqq", bufs=2, align_bytes=64)
-            pqs = wk.tile([P, 2 * P], U8, name="pqs", bufs=2, align_bytes=64)
+        def query_quantize(j):
+            n = 2 if j < QPAIRS else 1
+            pqq = wk.tile([P, 2, n, P], U32, name="pqq", bufs=2, align_bytes=64)
+            pqs = wk.tile([P, 2, n, P], U8, name="pqs", bufs=2, align_bytes=64)
             nc.vector.quantize_mx(
-                out=pqq[:].bitcast(FP8X4), scales=pqs[:],
-                in_=st["pq", m][:].rearrange("p s n t -> p (s n t)"),
+                out=pqq[:].rearrange("p s k n -> p (s k n)").bitcast(FP8X4),
+                scales=pqs[:].rearrange("p s k n -> p (s k n)"),
+                in_=st["pq", j][:].rearrange("p s n t -> p (s n t)"),
             )
-            st["pqq", m] = (pqq, pqs)
+            st["pqq", j] = (pqq, pqs)
 
         def read_product(m, h):
-            pqq, pqs = st["pqq", m]
+            j, k, n = qpair(m)
+            pqq, pqs = st["pqq", j]
             cb = ps.tile([P, 512], F32, name="cb", tag="cb", bufs=CB)
             for s in range(2):
                 nc.tensor.matmul_mx(
                     out=cb[:],
-                    lhsT=pqq[:, P * s : P * (s + 1)].bitcast(FP8X4),
-                    lhsT_scale=pqs[:, P * s : P * (s + 1)],
+                    lhsT=pqq[:, s, k, :].bitcast(FP8X4),
+                    lhsT_scale=pqs[:, s, k, :],
                     rhs=sw[:, s, 2048 * h : 2048 * (h + 1)].bitcast(FP8X4),
                     rhs_scale=ssc[:, s, 512 * h : 512 * (h + 1)],
                     start=(s == 0),
@@ -411,7 +432,8 @@ def tile_performer_state_step_f7_kernel(
         def update_start(n, h):
             s, a = divmod(n, 4)
             j, b = divmod(a, 2)
-            db = ps.tile([P, 512], F32, name="sd", bufs=SDB)
+            early = 2 * n + h in EARLY
+            db = ps.tile([P, 512], F32, name="sd", tag="cb" if early else "sd", bufs=CB if early else SDB)
             st["d", n, h] = db
             cols = slice(P * (2 * s + j), P * (2 * s + j + 1))
             nc.tensor.matmul_mx(
@@ -434,8 +456,42 @@ def tile_performer_state_step_f7_kernel(
                 rhs=vq[g][:, 512 * h : 512 * (h + 1)].bitcast(FP8X4),
                 rhs_scale=vsc[g][:, 512 * h : 512 * (h + 1)],
                 start=False,
-                stop=(g == TG - 1),
+                stop=(g == (1 if n < PARTIAL else TG - 1)),
             )
+
+        def part_out(n, h):
+            if ("nt", n) not in st:
+                ntp = wk.tile([P, D], F32, name="ntp", bufs=max(PARTIAL, 1))
+                st["nt", n] = ntp
+            dst = st["nt", n][:, 512 * h : 512 * (h + 1)]
+            if (n, h) in PART_ON_VECTOR:
+                nc.vector.tensor_copy(out=dst, in_=st["d", n, h][:])
+            else:
+                nc.scalar.copy(out=dst, in_=st["d", n, h][:])
+
+        def update_last(n, h):
+            s, a = divmod(n, 4)
+            g = TG - 1
+            cols = slice(512 * s + P * a, 512 * s + P * (a + 1))
+            db = ps.tile([P, 512], F32, name="sd", tag="sd", bufs=SDB)
+            nc.tensor.matmul_mx(
+                out=db[:],
+                lhsT=pkq[g][:, cols].bitcast(FP8X4),
+                lhsT_scale=pks[g][:, cols],
+                rhs=vq[g][:, 512 * h : 512 * (h + 1)].bitcast(FP8X4),
+                rhs_scale=vsc[g][:, 512 * h : 512 * (h + 1)],
+                start=True,
+                stop=True,
+            )
+            st["d", n, h] = db
+
+        def update_sum(n, h):
+            nt = st["nt", n]
+            part = nt[:, 512 * h : 512 * (h + 1)]
+            nc.vector.tensor_tensor(out=part, in0=st["d", n, h][:], in1=part, op=ALU.add)
+            if ("sum", n) in st:
+                nc.sync.dma_start(out=out_1[P * n : P * (n + 1), :], in_=nt[:])
+            st["sum", n] = 1
 
         def update_out(n, h):
             last = ("nt", n) in st
@@ -497,309 +553,311 @@ def tile_performer_state_step_f7_kernel(
 
 
         transposes(0)
-        write_abs()
         transposes(1)
-        copy_out(0)
-        copy_out(1)
+        write_abs()
         sign_and_scale()
-        write_clip()
+        copy_out(1)
+        copy_out(0)
         quantize_rows(0)
-        widen(3)
+        write_clip()
         quantize_rows(1)
+        widen(3)
+        widen(0)
         transposes(2)
-        permute_omega(1)
-        widen(1)
         write_ln()
         key_product(1)
-        transposes(3)
-        write_bias()
-        key_exp(1, 0)
-        key_exp(1, 1)
-        copy_out(2)
-        permute_scales(0)
-        permute_omega(0)
-        widen(2)
-        copy_out(3)
-        widen(0)
-        key_product(0)
-        transposes(6)
-        widen(5)
-        quantize_rows(2)
-        transposes(7)
-        key_exp(0, 1)
-        key_exp(0, 0)
-        transposes(5)
-        transposes(4)
-        copy_out(6)
-        decay_split()
-        copy_out(7)
-        key_product(2)
-        values_interleave(0)
-        key_exp(2, 0)
-        quantize_rows(4)
-        key_exp(2, 1)
-        copy_out(5)
-        key_product(3)
-        widen(7)
-        copy_out(4)
-        key_exp(3, 1)
-        widen(11)
         permute_scales(1)
-        decay_eye()
-        key_exp(3, 0)
-        key_product(7)
-        transposes(10)
-        transposes(11)
-        widen(4)
-        key_exp(7, 0)
-        quantize_rows(3)
-        features_interleave(0, 1)
-        key_exp(7, 1)
-        copy_out(11)
-        copy_out(10)
-        features_interleave(0, 0)
-        transposes(12)
-        copy_out(12)
-        decay_build()
-        features_quantize(0, 1)
+        write_bias()
+        widen(1)
+        permute_omega(1)
+        transposes(3)
+        key_exp(1, 0)
+        permute_omega(0)
+        key_exp(1, 1)
+        copy_out(3)
+        copy_out(2)
+        widen(2)
+        key_product(0)
+        key_exp(0, 1)
+        load_rows(2)
+        transposes(5)
+        key_exp(0, 0)
+        transposes(6)
+        quantize_rows(2)
+        widen(7)
+        key_product(2)
+        transposes(7)
+        values_interleave(0)
+        widen(8)
+        copy_out(5)
+        key_exp(2, 1)
+        values_quantize(0)
+        transposes(4)
         transposes(8)
-        decay_quantize()
-        key_product(6)
+        key_exp(2, 0)
+        copy_out(4)
+        copy_out(8)
+        key_product(3)
+        quantize_rows(3)
+        key_exp(3, 1)
+        transposes(9)
+        key_exp(3, 0)
+        decay_split()
+        copy_out(9)
+        key_product(4)
+        copy_out(7)
+        transposes(11)
+        key_exp(4, 0)
+        quantize_rows(5)
+        decay_eye()
+        load_rows(3)
+        key_exp(4, 1)
+        key_product(5)
+        copy_out(11)
+        copy_out(6)
+        key_exp(5, 1)
+        decay_build()
+        features_interleave(0, 0)
+        key_exp(5, 0)
+        transposes(10)
+        quantize_rows(4)
+        copy_out(10)
+        widen(5)
+        load_rows(4)
+        key_product(7)
+        key_exp(7, 0)
         transposes(13)
+        decay_quantize()
+        widen(6)
+        key_exp(7, 1)
+        widen(4)
+        decay_place()
+        widen(11)
+        key_product(6)
+        copy_out(13)
         key_exp(6, 0)
         key_exp(6, 1)
-        transposes(9)
-        values_quantize(0)
-        widen(6)
-        key_product(4)
-        copy_out(13)
         quantize_rows(6)
-        key_exp(4, 0)
-        key_exp(4, 1)
-        transposes(14)
-        quantize_rows(7)
-        key_product(5)
-        copy_out(9)
-        decay_place()
+        transposes(12)
         widen(10)
-        copy_out(14)
-        key_exp(5, 1)
-        key_exp(5, 0)
-        widen(8)
-        values_interleave(1)
-        query_product(0)
-        query_exp(0, 0)
-        query_exp(0, 1)
+        copy_out(12)
         key_product(10)
-        features_quantize(0, 0)
-        values_quantize(1)
-        widen(9)
-        key_exp(10, 0)
         key_exp(10, 1)
-        transposes(15)
-        update_start(0, 0)
-        key_product(11)
-        copy_out(8)
-        copy_out(15)
-        features_interleave(1, 0)
-        query_scale(0)
-        transposes(16)
-        key_exp(11, 1)
-        quantize_rows(5)
-        key_exp(11, 0)
-        update_start(0, 1)
-        copy_out(16)
-        key_product(9)
-        key_exp(9, 0)
-        transposes(17)
-        update_add(0, 0, 0)
-        features_quantize(1, 0)
-        key_exp(9, 1)
-        query_quantize(0)
-        copy_out(17)
-        read_product(0, 1)
-        values_interleave(2)
-        key_product(8)
-        read_square(0, 1)
-        update_add(0, 1, 0)
-        quantize_rows(8)
-        transposes(18)
-        values_quantize(2)
-        read_product(0, 0)
-        key_exp(8, 0)
-        key_exp(8, 1)
-        update_add(0, 1, 1)
-        copy_out(18)
-        query_product(2)
-        read_square(0, 0)
-        query_exp(2, 1)
-        features_interleave(2, 0)
-        features_quantize(2, 0)
-        transposes(19)
-        update_add(0, 0, 1)
-        query_exp(2, 0)
-        copy_out(19)
-        update_add(0, 0, 2)
-        update_out(0, 0)
-        query_product(1)
-        update_add(0, 1, 2)
-        features_interleave(1, 1)
-        update_start(2, 0)
-        update_add(2, 0, 0)
-        update_out(0, 1)
-        query_exp(1, 1)
-        update_add(2, 0, 1)
-        query_scale(2)
-        query_exp(1, 0)
-        quantize_rows(10)
-        update_add(2, 0, 2)
-        read_norm(0)
-        update_start(2, 1)
-        update_out(2, 0)
-        update_add(2, 1, 0)
-        query_quantize(2)
-        update_add(2, 1, 1)
-        update_add(2, 1, 2)
-        update_out(2, 1)
-        query_product(3)
-        read_product(2, 0)
-        read_out(0, 0)
+        permute_scales(0)
         update_start(1, 0)
-        quantize_rows(9)
-        update_add(1, 0, 0)
-        query_scale(1)
-        update_add(1, 0, 1)
-        query_exp(3, 0)
-        read_out(0, 1)
-        query_exp(3, 1)
-        update_start(3, 0)
-        update_add(1, 0, 2)
-        update_add(3, 0, 0)
-        read_product(2, 1)
-        update_add(3, 0, 1)
-        read_square(2, 0)
-        query_quantize(1)
-        update_out(1, 0)
-        query_product(4)
+        features_quantize(0, 0)
+        key_exp(10, 0)
         update_start(1, 1)
-        update_add(3, 0, 2)
+        key_product(8)
+        update_start(2, 0)
+        widen(9)
+        values_interleave(1)
+        load_rows(5)
+        key_exp(8, 0)
+        update_start(0, 1)
+        key_exp(8, 1)
+        update_start(2, 1)
+        features_interleave(1, 0)
+        values_quantize(1)
+        load_rows(6)
+        transposes(14)
         update_add(1, 1, 0)
-        read_square(2, 1)
-        query_exp(4, 1)
-        features_quantize(1, 1)
-        read_norm(2)
+        key_product(9)
+        update_add(2, 1, 0)
+        copy_out(14)
+        update_add(0, 1, 0)
+        key_exp(9, 0)
+        transposes(15)
+        features_quantize(1, 0)
+        update_start(0, 0)
+        key_exp(9, 1)
+        update_add(0, 0, 0)
+        key_product(11)
         update_add(1, 1, 1)
-        query_exp(4, 0)
-        query_scale(3)
-        features_interleave(2, 1)
+        copy_out(15)
+        key_exp(11, 0)
+        update_add(2, 1, 1)
+        key_exp(11, 1)
+        quantize_rows(7)
+        transposes(16)
+        update_add(0, 1, 1)
+        update_add(1, 0, 0)
+        copy_out(16)
+        values_interleave(2)
+        query_product(0)
+        features_interleave(2, 0)
+        query_exp(0, 1)
+        values_quantize(2)
+        update_add(0, 0, 1)
+        features_quantize(2, 0)
+        update_add(1, 0, 1)
+        query_exp(0, 0)
+        transposes(17)
+        copy_out(17)
+        update_add(2, 0, 0)
+        load_rows(7)
+        query_product(1)
+        query_exp(1, 0)
+        update_add(2, 0, 1)
+        quantize_rows(8)
+        update_add(2, 0, 2)
+        query_scale(0)
+        update_add(1, 0, 2)
         update_add(1, 1, 2)
-        read_product(1, 0)
-        update_out(3, 0)
-        read_product(1, 1)
-        query_product(5)
-        update_start(3, 1)
+        query_exp(1, 1)
+        update_add(0, 1, 2)
+        update_add(2, 1, 2)
+        update_out(1, 0)
+        query_quantize(0)
         update_out(1, 1)
-        read_square(1, 0)
-        read_square(1, 1)
-        query_quantize(3)
-        read_out(2, 0)
-        update_add(3, 1, 0)
-        query_exp(5, 0)
-        update_add(3, 1, 1)
-        update_add(3, 1, 2)
-        read_out(2, 1)
-        query_exp(5, 1)
-        update_out(3, 1)
-        read_product(3, 1)
-        read_square(3, 1)
-        query_scale(4)
-        read_norm(1)
+        query_scale(1)
+        update_add(0, 0, 2)
+        update_out(2, 0)
+        features_interleave(2, 1)
+        query_product(2)
+        transposes(18)
+        read_product(0, 0)
+        update_out(2, 1)
+        read_product(0, 1)
+        quantize_rows(9)
+        query_exp(2, 1)
+        query_exp(2, 0)
+        read_square(0, 0)
+        update_start(3, 0)
+        query_quantize(1)
         features_quantize(2, 1)
-        update_start(4, 0)
-        read_product(3, 0)
-        query_product(6)
-        update_start(5, 0)
-        update_add(4, 0, 0)
-        query_quantize(4)
-        read_square(3, 0)
-        query_exp(6, 1)
-        query_exp(6, 0)
-        update_add(4, 0, 1)
-        update_add(5, 0, 0)
+        update_out(0, 0)
+        update_add(3, 0, 0)
+        read_square(0, 1)
+        query_product(3)
+        update_add(3, 0, 1)
+        query_scale(2)
+        update_add(3, 0, 2)
+        update_out(0, 1)
+        update_start(3, 1)
+        copy_out(18)
+        update_add(3, 1, 0)
+        read_norm(0)
+        read_product(1, 0)
+        read_out(0, 0)
+        query_quantize(2)
+        read_out(0, 1)
+        query_exp(3, 0)
+        query_exp(3, 1)
+        update_add(3, 1, 1)
+        read_square(1, 0)
+        read_product(1, 1)
+        update_add(3, 1, 2)
+        query_product(4)
+        transposes(19)
+        read_square(1, 1)
+        query_scale(3)
+        read_product(2, 0)
+        read_norm(1)
+        query_quantize(3)
+        update_out(3, 0)
         read_out(1, 0)
-        update_add(4, 0, 2)
-        read_product(4, 0)
-        read_norm(3)
+        read_product(2, 1)
         read_out(1, 1)
-        read_product(4, 1)
-        update_out(4, 0)
-        query_product(7)
-        read_square(4, 0)
-        update_add(5, 0, 1)
+        query_exp(4, 1)
+        query_exp(4, 0)
+        update_start(4, 0)
+        read_square(2, 0)
+        read_square(2, 1)
+        update_add(4, 0, 0)
+        update_add(4, 0, 1)
+        query_scale(4)
+        query_product(5)
+        update_out(3, 1)
+        update_add(4, 0, 2)
+        copy_out(19)
+        read_norm(2)
         update_start(4, 1)
+        query_exp(5, 0)
+        read_product(3, 0)
+        query_exp(5, 1)
+        quantize_rows(10)
+        read_square(3, 0)
+        read_product(3, 1)
         update_add(4, 1, 0)
+        read_square(3, 1)
+        query_quantize(4)
+        read_norm(3)
+        read_out(2, 0)
+        read_out(2, 1)
         query_scale(5)
-        read_out(3, 0)
-        read_square(4, 1)
-        read_norm(4)
-        query_exp(7, 0)
-        update_add(5, 0, 2)
         query_quantize(5)
         update_add(4, 1, 1)
-        query_exp(7, 1)
-        update_out(5, 0)
-        read_out(3, 1)
         update_add(4, 1, 2)
-        query_scale(6)
-        read_product(5, 0)
-        read_square(5, 0)
-        read_product(5, 1)
+        query_product(6)
+        read_product(4, 0)
+        update_out(4, 0)
+        update_start(5, 0)
+        query_exp(6, 0)
+        read_product(4, 1)
+        update_add(5, 0, 0)
+        read_out(3, 0)
+        read_out(3, 1)
+        update_add(5, 0, 1)
+        query_exp(6, 1)
+        read_square(4, 0)
+        update_add(5, 0, 2)
+        read_square(4, 1)
         update_out(4, 1)
-        read_out(4, 0)
+        query_product(7)
+        update_out(5, 0)
+        read_product(5, 0)
+        query_scale(6)
+        read_product(5, 1)
+        read_norm(4)
+        read_square(5, 0)
         update_start(5, 1)
         read_square(5, 1)
-        update_add(5, 1, 0)
-        update_add(5, 1, 1)
+        query_exp(7, 0)
         query_quantize(6)
+        update_add(5, 1, 0)
+        read_norm(5)
+        read_out(4, 0)
+        update_add(5, 1, 1)
         update_start(6, 0)
-        update_add(5, 1, 2)
-        read_product(6, 0)
-        read_out(4, 1)
-        read_product(6, 1)
         update_add(6, 0, 0)
+        read_out(4, 1)
+        query_exp(7, 1)
+        update_add(5, 1, 2)
+        query_scale(7)
+        read_product(6, 1)
+        read_product(6, 0)
+        read_out(5, 0)
+        update_add(6, 0, 1)
         update_out(5, 1)
+        query_quantize(7)
+        read_square(6, 1)
         update_start(6, 1)
         update_add(6, 1, 0)
-        update_add(6, 0, 1)
         update_add(6, 0, 2)
-        read_norm(5)
         read_square(6, 0)
-        query_scale(7)
-        read_square(6, 1)
-        update_out(6, 0)
         update_add(6, 1, 1)
-        update_add(6, 1, 2)
-        read_out(5, 0)
-        query_quantize(7)
         read_out(5, 1)
-        read_product(7, 0)
-        update_out(6, 1)
+        update_out(6, 0)
+        update_add(6, 1, 2)
         read_product(7, 1)
-        read_norm(6)
+        update_out(6, 1)
+        read_product(7, 0)
         update_start(7, 0)
-        read_square(7, 0)
-        update_add(7, 0, 0)
-        update_add(7, 0, 1)
-        read_square(7, 1)
-        update_add(7, 0, 2)
-        read_out(6, 0)
         update_start(7, 1)
+        update_add(7, 0, 0)
         update_add(7, 1, 0)
-        read_norm(7)
+        read_square(7, 1)
+        update_add(7, 0, 1)
+        update_add(7, 0, 2)
+        read_square(7, 0)
+        read_norm(6)
         update_add(7, 1, 1)
+        read_norm(7)
+        read_out(6, 0)
+        update_add(7, 1, 2)
         read_out(6, 1)
         update_out(7, 0)
-        update_add(7, 1, 2)
         update_out(7, 1)
         read_out(7, 1)
         read_out(7, 0)

from contextlib import ExitStack

import concourse.mybir as mybir
from concourse.masks import make_identity

F32 = mybir.dt.float32
BF16 = mybir.dt.bfloat16
I32 = mybir.dt.int32
U32 = mybir.dt.uint32
U8 = mybir.dt.uint8
FP8 = mybir.dt.float8_e4m3fn
FP8X4 = mybir.dt.float8_e4m3fn_x4
FP4X4 = mybir.dt.float4_e2m1fn_x4
ACTF = mybir.ActivationFunctionType
ALU = mybir.AluOpType

P = 128
M, T, K, R, F, D = 1024, 1536, 1024, 512, 1024, 1024
EPS = 1e-6
FLOPS = 2 * (M * K * R + T * K * R + M * F * D + T * F * D)

TPB, ABB, CB, SDB = 1,1,4,2
KEY_TURNS = 8
EARLY = (0, 1, 2, 3)
UPDATE_ON_VECTOR = ((0, 0), (1, 0), (6, 1))
PART_ON_VECTOR = ()
COPY_ON_VECTOR = (1,)
WIDEN_ON_VECTOR = (1, 2, 3, 6, 8, 11)
SINGLES = 2
XTB = 2
ROWB = 14
MERGED = 2
QPAIRS = 0
PARTIAL = 0
KG = K // 512
TG = T // 512
FG = F // 512


def tile_performer_state_step_f7_kernel(
    tc, queries, keys, values_bytes, values_scale, omega_words, omega_scales,
    state_words, state_scales, half_norm, read, write, keep, gain, out_0, out_1,
):
    nc = tc.nc
    with ExitStack() as ctx:
        cst = ctx.enter_context(tc.tile_pool(name="cst", bufs=1))
        raw = ctx.enter_context(tc.tile_pool(name="raw", bufs=1))
        wk = ctx.enter_context(tc.tile_pool(name="wk", bufs=3))
        ps = ctx.enter_context(tc.psum_pool(name="ps", bufs=2))
        ctx.enter_context(tc.manual_schedule())

        kview = keys.rearrange("(g p t) k -> g t p k", p=P, t=4)
        kraw = []
        for i in range(12):
            kr = raw.tile([P, K], BF16, name="rows", bufs=ROWB, align_bytes=64)
            kraw.append(kr)
        qraw = []
        vbytes = []
        for g in range(TG):
            vb = raw.tile([P, 4, D], U8, name=f"vbytes{g}", align_bytes=64)
            vbytes.append(vb)

        ow = cst.tile([P, KG, 2 * R], U8, name="ow", align_bytes=64)
        osc = cst.tile([P, KG, R], U8, name="osc", align_bytes=64)
        sw = cst.tile([P, FG, 4 * D], U8, name="sw", align_bytes=64)
        ssc = cst.tile([P, FG, D], U8, name="ssc", align_bytes=64)
        wr = cst.tile([P, TG, 4], BF16, name="wr")
        hn = cst.tile([P, TG, 4], BF16, name="hn")
        vs = cst.tile([P, TG, 4], F32, name="vs")
        rd = cst.tile([P, FG, 4], BF16, name="rd")
        kk = cst.tile([P, 2, 2, 4], BF16, name="kk")
        sd = cst.tile([P, FG, 2, 4 * D], U8, name="sd", align_bytes=64)
        sds = cst.tile([P, FG, 2, D], U8, name="sds", align_bytes=64)
        gn = cst.tile([P, D], BF16, name="gn")

        quarter = cst.tile([P, TG * 4], F32, name="quarter")
        mhalf = cst.tile([P, 1], F32, name="mhalf")
        mask = cst.tile([P, 8], I32, name="mask")
        one = cst.tile([P, 1], F32, name="one")
        dk = cst.tile([P, 4, 32, 16], BF16, name="dk", align_bytes=64)
        dz = cst.tile([P, 2, 4 * P], U32, name="dz", align_bytes=64)
        nc.vector.memset(osc[:].bitcast(I32), 0)
        nc.vector.memset(one[:], 1.0)
        nc.vector.memset(quarter[:], 0.25)
        nc.vector.memset(mhalf[:], -0.5)
        nc.vector.memset(mask[:], -983056)
        identf = cst.tile([P, P], F32, name="identf")
        make_identity(nc, identf[:])
        nc.vector.memset(ssc[:].bitcast(I32), 0)
        nc.vector.memset(sds[:].rearrange("p s j n -> p (s j n)").bitcast(I32), 0)

        vview = values_bytes.rearrange("(g p t) d -> g p t d", p=P, t=4)
        oview = omega_scales.rearrange("g (q r) n -> r q g n", r=4)
        sview = state_scales.rearrange("g (q r) n -> r q g n", r=4)
        nc.scalar.dma_start(out=wr[:], in_=write.rearrange("(g p t) -> p g t", p=P, t=4))
        nc.scalar.dma_start(out=vs[:], in_=values_scale.rearrange("(g p t) o -> p g (t o)", p=P, t=4))
        nc.scalar.dma_start(out=hn[:], in_=half_norm.rearrange("(g p t) -> p g t", p=P, t=4))
        nc.sync.dma_start(out=kraw[0][:], in_=kview[0, 0])
        nc.sync.dma_start(out=kraw[1][:], in_=kview[0, 1])
        nc.sync.dma_start(out=vbytes[0][:], in_=vview[0])
        nc.sync.dma_start(out=ow[:], in_=omega_words.rearrange("g p b -> p g b"))
        for r in range(4):
            nc.sync.dma_start(out=osc[r:P:32, :, :].bitcast(I32), in_=oview[r].bitcast(I32))
        nc.sync.dma_start(out=kraw[2][:], in_=kview[0, 2])
        nc.sync.dma_start(out=kraw[3][:], in_=kview[0, 3])
        nc.sync.dma_start(out=vbytes[1][:], in_=vview[1])
        for t in range(4):
            nc.sync.dma_start(out=kraw[4 + t][:], in_=kview[1, t])
        nc.sync.dma_start(out=rd[:], in_=read.rearrange("(g p t) -> p g t", p=P, t=4))
        kview4 = keep.rearrange("(s j b r t) -> b r s j t", s=2, j=2, b=2, r=32)
        for q in range(4):
            nc.sync.dma_start(out=kk[32 * q : 32 * (q + 1)], in_=kview4[q // 2])
        nc.sync.dma_start(out=vbytes[2][:], in_=vview[2])
        for t in range(4):
            nc.sync.dma_start(out=kraw[8 + t][:], in_=kview[2, t])
        nc.sync.dma_start(out=sw[:], in_=state_words.rearrange("g p n t -> p g (n t)"))
        for r in range(4):
            nc.sync.dma_start(out=ssc[r:P:32, :, :].bitcast(I32), in_=sview[r].bitcast(I32))
        for m in range(ROWB - 12):
            qr = raw.tile([P, K], BF16, name="rows", bufs=ROWB, align_bytes=64)
            qraw.append(qr)
            nc.sync.dma_start(out=qr[:], in_=queries[P * m : P * (m + 1), :])
        wview = state_words.rearrange("s (j b r) n t -> s j b r (n t)", j=2, b=2)
        for s in range(FG):
            for j in range(2):
                for q in range(4):
                    nc.sync.dma_start(
                        out=sd[32 * q : 32 * (q + 1), s, j].bitcast(I32), in_=wview[s, j, q // 2].bitcast(I32)
                    )
        for q in range(4):
            nc.sync.dma_start(
                out=sds[32 * q : 32 * q + 4].bitcast(I32),
                in_=state_scales.rearrange("s (j b r) n -> b r s j n", j=2, b=2)[q // 2].bitcast(I32),
            )
        nc.sync.dma_start(out=gn[:], in_=gain.partition_broadcast(P))

        kbias = cst.tile([P, TG * 4], F32, name="kbias")
        vss = cst.tile([P, TG * 4], F32, name="vss")

        klow = cst.tile([P, 2, 2, 4], BF16, name="klow")
        eye = cst.tile([P, 32], BF16, name="eye")
        dcod = cst.tile([P, 4 * P], U32, name="dcod", align_bytes=64)
        dsc = cst.tile([P, 4 * P], U8, name="dsc", align_bytes=64)
        spare = cst.tile([P, 1], F32, name="spare")
        nc.scalar.activation(out=spare[:], in_=one[:], func=ACTF.Ln)
        nc.vector.memset(dz[:].bitcast(I32), 0)
        nc.vector.memset(dk[:].rearrange("p c r x -> p (c r x)").bitcast(F32), 0.0)

        owp = cst.tile([P, KG, 4, P, 2], U8, name="owp", align_bytes=64)
        osp = cst.tile([P, KG, 4, P], U8, name="osp", align_bytes=64)
        pkq, pks, vq, vsc = [], [], [], []
        for g in range(TG):
            a = cst.tile([P, F], U32, name=f"pkq{g}", align_bytes=64)
            b = cst.tile([P, F], U8, name=f"pks{g}", align_bytes=64)
            c = cst.tile([P, D], U32, name=f"vq{g}", align_bytes=64)
            d = cst.tile([P, D], U8, name=f"vsc{g}", align_bytes=64)
            pkq.append(a)
            pks.append(b)
            vq.append(c)
            vsc.append(d)
        st = {}

        def load_rows(m):
            qr = raw.tile([P, K], BF16, name="rows", bufs=ROWB, align_bytes=64)
            qraw.append(qr)
            nc.sync.dma_start(out=qr[:], in_=queries[P * m : P * (m + 1), :])

        def rows(i):
            return kraw[i] if i < 12 else qraw[i - 12]

        def transposes(i):
            words = rows(i)[:].bitcast(F32)
            early = i < KEY_TURNS
            tp = ps.tile([P, KG, 2, P], F32, name="tp", tag="cb" if early else "tp", bufs=CB if early else TPB)
            for g in range(KG):
                for u in range(2):
                    nc.tensor.transpose(
                        tp[:, g, u, :], words[:, 256 * g + u : 256 * (g + 1) : 2], identf[:]
                    )
            st["tp", i] = tp

        def pair(i):
            if i < SINGLES:
                return i, 0
            return SINGLES + (i - SINGLES) // 2, (i - SINGLES) % 2

        def copy_out(i):
            j, n = pair(i)
            if ("xt", j) not in st:
                xt = wk.tile([P, 2 * KG * P * 4], BF16, name="xt", bufs=XTB, align_bytes=64)
                st["xt", j] = xt
            dst = st["xt", j][:, 1024 * n : 1024 * (n + 1)].bitcast(F32).rearrange("p (g r u) -> p g r u", g=KG, u=2)
            src = st["tp", i][:].rearrange("p g u r -> p g r u")
            if i in COPY_ON_VECTOR:
                nc.vector.tensor_copy(out=dst, in_=src)
            else:
                nc.scalar.copy(out=dst, in_=src)

        def quantize_rows(j):
            n = 1 if j < SINGLES else 2
            xq = wk.tile([P, 2 * KG * P], U32, name="xq", bufs=3, align_bytes=64)
            xs = wk.tile([P, 2 * KG * P], U8, name="xs", bufs=3, align_bytes=64)
            nc.vector.quantize_mx(
                out=xq[:, 0 : 256 * n].bitcast(FP8X4), scales=xs[:, 0 : 256 * n],
                in_=st["xt", j][:, 0 : 1024 * n],
            )
            for k in range(n):
                i = j if n == 1 else SINGLES + 2 * (j - SINGLES) + k
                st["xq", i] = (xq[:, 256 * k : 256 * (k + 1)], xs[:, 256 * k : 256 * (k + 1)])

        def widen(i):
            g, t = divmod(i, 4)
            if ("vpl", g) not in st:
                vpl = wk.tile([P, 4, D], BF16, name="vpl", bufs=2, align_bytes=64)
                st["vpl", g] = vpl
            dst = st["vpl", g][:, t, :]
            src = vbytes[g][:, t, :].bitcast(FP8)
            if i in WIDEN_ON_VECTOR:
                nc.vector.tensor_scalar(
                    out=dst, in0=src, scalar1=vss[:, i : i + 1], scalar2=None, op0=ALU.mult
                )
            else:
                nc.scalar.activation(out=dst, in_=src, func=ACTF.Copy, scale=vss[:, i : i + 1])

        def interleave(dst, planes):
            nc.vector.tensor_copy(
                out=dst.rearrange("p (c i t) -> p c t i", i=4, t=4),
                in_=planes.rearrange("p t (c i) -> p c t i", i=4),
            )

        def values_interleave(g):
            vint = wk.tile([P, D * 4], BF16, name="inter", bufs=2, align_bytes=64)
            interleave(vint[:], st["vpl", g][:])
            st["vint", g] = vint

        def values_quantize(g):
            nc.vector.quantize_mx(
                out=vq[g][:].bitcast(FP8X4), scales=vsc[g][:], in_=st["vint", g][:]
            )

        def key_product(i):
            kq, ks = st["xq", i]
            bank = ps.tile([P, R], F32, name="ab", bufs=ABB)
            for c in range(KG):
                nc.tensor.matmul_mx(
                    out=bank[:],
                    lhsT=kq[:, P * c : P * (c + 1)].bitcast(FP8X4),
                    lhsT_scale=ks[:, P * c : P * (c + 1)],
                    rhs=ow[:, c, :].bitcast(FP4X4),
                    rhs_scale=osc[:, c, :],
                    start=(c == 0),
                    stop=(c == KG - 1),
                )
            st["b", i] = bank

        def key_exp(i, s):
            g, t = divmod(i, 4)
            if ("pl", g) not in st:
                pl = wk.tile([P, 4, 2 * R], BF16, name="pl", bufs=2, align_bytes=64)
                st["pl", g] = pl
            nc.scalar.activation(
                out=st["pl", g][:, t, R * s : R * (s + 1)], in_=st["b", i][:], func=ACTF.Exp,
                bias=kbias[:, i : i + 1], scale=1.0 - 2.0 * s,
            )

        def features_interleave(g, s):
            cols = slice(0, 2 * R) if g < MERGED else slice(R * s, R * (s + 1))
            pint = wk.tile([P, 2 * R * 4], BF16, name="inter", bufs=2, align_bytes=64)
            pint = pint[:, 0 : 4 * (cols.stop - cols.start)]
            interleave(pint, st["pl", g][:, :, cols])
            st["pint", g, s] = pint, cols

        def features_quantize(g, s):
            pint, cols = st["pint", g, s]
            nc.vector.quantize_mx(
                out=pkq[g][:, cols].bitcast(FP8X4), scales=pks[g][:, cols], in_=pint
            )

        def permute_omega(c):
            nc.vector.tensor_copy(
                out=owp[:, c], in_=ow[:, c].rearrange("p (m t b) -> p t m b", t=4, b=2)
            )

        def permute_scales(c):
            nc.vector.tensor_copy(
                out=osp[:, c], in_=osc[:, c].rearrange("p (m t) -> p t m", t=4)
            )

        def query_product(m):
            qq, qs = st["xq", 12 + m]
            bank = ps.tile([P, 4, P], F32, name="ab", bufs=ABB)
            for t in range(4):
                for c in range(KG):
                    nc.tensor.matmul_mx(
                        out=bank[:, t, :],
                        lhsT=owp[:, c, t].rearrange("p m b -> p (m b)").bitcast(FP4X4),
                        lhsT_scale=osp[:, c, t, :],
                        rhs=qq[:, P * c : P * (c + 1)].bitcast(FP8X4),
                        rhs_scale=qs[:, P * c : P * (c + 1)],
                        start=(c == 0),
                        stop=(c == KG - 1),
                    )
            st["a", m] = bank

        def qpair(m):
            if m < 2 * QPAIRS:
                return m // 2, m % 2, 2
            return m - QPAIRS, 0, 1

        def query_exp(m, s):
            j, k, n = qpair(m)
            if ("ex", j) not in st:
                ex = wk.tile([P, 2, n, P, 4], F32, name="ex", bufs=2)
                st["ex", j] = ex
            nc.scalar.activation(
                out=st["ex", j][:, s, k], in_=st["a", m][:].rearrange("p t n -> p n t"), func=ACTF.Exp,
                scale=1.0 - 2.0 * s,
            )

        def query_scale(j):
            n = 2 if j < QPAIRS else 1
            pq = wk.tile([P, 2, n * P, 4], BF16, name="pq", bufs=2, align_bytes=64)
            nc.vector.tensor_tensor(
                out=pq[:], in0=st["ex", j][:].rearrange("p s k n t -> p s (k n) t"),
                in1=rd[:].unsqueeze(2).to_broadcast([P, 2, n * P, 4]), op=ALU.mult,
            )
            st["pq", j] = pq

        def query_quantize(j):
            n = 2 if j < QPAIRS else 1
            pqq = wk.tile([P, 2, n, P], U32, name="pqq", bufs=2, align_bytes=64)
            pqs = wk.tile([P, 2, n, P], U8, name="pqs", bufs=2, align_bytes=64)
            nc.vector.quantize_mx(
                out=pqq[:].rearrange("p s k n -> p (s k n)").bitcast(FP8X4),
                scales=pqs[:].rearrange("p s k n -> p (s k n)"),
                in_=st["pq", j][:].rearrange("p s n t -> p (s n t)"),
            )
            st["pqq", j] = (pqq, pqs)

        def read_product(m, h):
            j, k, n = qpair(m)
            pqq, pqs = st["pqq", j]
            cb = ps.tile([P, 512], F32, name="cb", tag="cb", bufs=CB)
            for s in range(2):
                nc.tensor.matmul_mx(
                    out=cb[:],
                    lhsT=pqq[:, s, k, :].bitcast(FP8X4),
                    lhsT_scale=pqs[:, s, k, :],
                    rhs=sw[:, s, 2048 * h : 2048 * (h + 1)].bitcast(FP8X4),
                    rhs_scale=ssc[:, s, 512 * h : 512 * (h + 1)],
                    start=(s == 0),
                    stop=(s == 1),
                )
            st["c", m, h] = cb

        def read_square(m, h):
            if ("sq", m) not in st:
                sq = wk.tile([P, 2], F32, name="sq", bufs=2)
                st["sq", m] = sq
            junk = wk.tile([P, 512], BF16, name="junk", bufs=2)
            nc.scalar.activation(
                out=junk[:], in_=st["c", m, h][:], func=ACTF.Square, scale=1.0 / 32.0,
                accum_out=st["sq", m][:, h : h + 1],
            )

        def read_norm(m):
            sq = st["sq", m]
            ms = wk.tile([P, 1], F32, name="ms", bufs=2)
            nc.gpsimd.tensor_scalar(
                out=ms[:], in0=sq[:, 0:1], scalar1=sq[:, 1:2], scalar2=EPS, op0=ALU.add, op1=ALU.add
            )
            rstd = wk.tile([P, 1], F32, name="rstd", bufs=2)
            nc.gpsimd.tensor_tensor(out=rstd[:], in0=ms[:], in1=mhalf[:], op=ALU.pow)
            st["rstd", m] = rstd

        def read_out(m, h):
            last = ("yt", m) in st
            if not last:
                yt = wk.tile([P, D], F32, name="yt", bufs=3)
                st["yt", m] = yt
            yt = st["yt", m]
            nc.vector.scalar_tensor_tensor(
                out=yt[:, 512 * h : 512 * (h + 1)], in0=st["c", m, h][:],
                scalar=st["rstd", m][:], in1=gn[:, 512 * h : 512 * (h + 1)],
                op0=ALU.mult, op1=ALU.mult,
            )
            if m == 7:
                nc.sync.dma_start(
                    out=out_0[P * m : P * (m + 1), 512 * h : 512 * (h + 1)], in_=yt[:, 512 * h : 512 * (h + 1)]
                )
            elif last:
                nc.sync.dma_start(out=out_0[P * m : P * (m + 1), :], in_=yt[:])

        def decay_eye():
            half = wk.tile([P, 64], F32, name="half", bufs=1)
            nc.gpsimd.tensor_tensor(out=half[:], in0=identf[:, 0:64], in1=identf[:, 64:128], op=ALU.add)
            nc.gpsimd.tensor_tensor(out=eye[:], in0=half[:, 0:32], in1=half[:, 32:64], op=ALU.add)

        def decay_split():
            flat = kk[:].rearrange("p s j t -> p (s j t)")
            khi = cst.tile([P, 16], BF16, name="khi")
            nc.vector.tensor_tensor(
                out=khi[:].bitcast(I32), in0=flat.bitcast(I32), in1=mask[:], op=ALU.bitwise_and
            )
            low = klow[:].rearrange("p s j t -> p (s j t)")
            nc.vector.tensor_tensor(out=low, in0=flat, in1=khi[:], op=ALU.subtract)
            for q in (0, 2):
                nc.vector.tensor_copy(
                    out=low[32 * q : 32 * (q + 1)], in_=khi[32 * q : 32 * (q + 1), :]
                )

        def decay_build():
            nc.vector.tensor_tensor(
                out=dk[:, :, :, 0:16:5],
                in0=eye[:].unsqueeze(1).unsqueeze(3).to_broadcast([P, 4, 32, 4]),
                in1=klow[:].rearrange("p s j t -> p (s j) t").unsqueeze(2).to_broadcast([P, 4, 32, 4]),
                op=ALU.mult,
            )

        def decay_quantize():
            nc.vector.quantize_mx(
                out=dcod[:].bitcast(FP8X4), scales=dsc[:], in_=dk[:].rearrange("p c r x -> p (c r x)")
            )

        def decay_place():
            for b in range(2):
                nc.vector.tensor_copy(
                    out=dz[64 * b : 64 * (b + 1), b, :].bitcast(I32),
                    in_=dcod[64 * b : 64 * (b + 1), :].bitcast(I32),
                )

        def update_start(n, h):
            s, a = divmod(n, 4)
            j, b = divmod(a, 2)
            early = 2 * n + h in EARLY
            db = ps.tile([P, 512], F32, name="sd", tag="cb" if early else "sd", bufs=CB if early else SDB)
            st["d", n, h] = db
            cols = slice(P * (2 * s + j), P * (2 * s + j + 1))
            nc.tensor.matmul_mx(
                out=db[:],
                lhsT=dz[:, b, cols].bitcast(FP8X4),
                lhsT_scale=dsc[:, cols],
                rhs=sd[:, s, j, 2048 * h : 2048 * (h + 1)].bitcast(FP8X4),
                rhs_scale=sds[:, s, j, 512 * h : 512 * (h + 1)],
                start=True,
                stop=False,
            )

        def update_add(n, h, g):
            s, a = divmod(n, 4)
            cols = slice(512 * s + P * a, 512 * s + P * (a + 1))
            nc.tensor.matmul_mx(
                out=st["d", n, h][:],
                lhsT=pkq[g][:, cols].bitcast(FP8X4),
                lhsT_scale=pks[g][:, cols],
                rhs=vq[g][:, 512 * h : 512 * (h + 1)].bitcast(FP8X4),
                rhs_scale=vsc[g][:, 512 * h : 512 * (h + 1)],
                start=False,
                stop=(g == (1 if n < PARTIAL else TG - 1)),
            )

        def part_out(n, h):
            if ("nt", n) not in st:
                ntp = wk.tile([P, D], F32, name="ntp", bufs=max(PARTIAL, 1))
                st["nt", n] = ntp
            dst = st["nt", n][:, 512 * h : 512 * (h + 1)]
            if (n, h) in PART_ON_VECTOR:
                nc.vector.tensor_copy(out=dst, in_=st["d", n, h][:])
            else:
                nc.scalar.copy(out=dst, in_=st["d", n, h][:])

        def update_last(n, h):
            s, a = divmod(n, 4)
            g = TG - 1
            cols = slice(512 * s + P * a, 512 * s + P * (a + 1))
            db = ps.tile([P, 512], F32, name="sd", tag="sd", bufs=SDB)
            nc.tensor.matmul_mx(
                out=db[:],
                lhsT=pkq[g][:, cols].bitcast(FP8X4),
                lhsT_scale=pks[g][:, cols],
                rhs=vq[g][:, 512 * h : 512 * (h + 1)].bitcast(FP8X4),
                rhs_scale=vsc[g][:, 512 * h : 512 * (h + 1)],
                start=True,
                stop=True,
            )
            st["d", n, h] = db

        def update_sum(n, h):
            nt = st["nt", n]
            part = nt[:, 512 * h : 512 * (h + 1)]
            nc.vector.tensor_tensor(out=part, in0=st["d", n, h][:], in1=part, op=ALU.add)
            if ("sum", n) in st:
                nc.sync.dma_start(out=out_1[P * n : P * (n + 1), :], in_=nt[:])
            st["sum", n] = 1

        def update_out(n, h):
            last = ("nt", n) in st
            if not last:
                nt = wk.tile([P, D], F32, name="nt", bufs=2)
                st["nt", n] = nt
            nt = st["nt", n]
            if (n, h) in UPDATE_ON_VECTOR:
                nc.vector.tensor_copy(out=nt[:, 512 * h : 512 * (h + 1)], in_=st["d", n, h][:])
            else:
                nc.scalar.copy(out=nt[:, 512 * h : 512 * (h + 1)], in_=st["d", n, h][:])
            if n == 7:
                nc.sync.dma_start(
                    out=out_1[P * n : P * (n + 1), 512 * h : 512 * (h + 1)], in_=nt[:, 512 * h : 512 * (h + 1)]
                )
            elif last:
                nc.sync.dma_start(out=out_1[P * n : P * (n + 1), :], in_=nt[:])

        def sign_and_scale():
            wflat = wr[:].rearrange("p g t -> p (g t)")
            wlt = cst.tile([P, TG * 4], F32, name="wlt")
            nc.vector.tensor_scalar(out=wlt[:], in0=wflat, scalar1=0.0, scalar2=None, op0=ALU.is_lt)
            wsgn = cst.tile([P, TG * 4], F32, name="wsgn")
            nc.vector.scalar_tensor_tensor(
                out=wsgn[:], in0=wflat, scalar=0.0, in1=wlt[:], op0=ALU.is_gt, op1=ALU.subtract,
            )
            nc.vector.tensor_tensor(
                out=vss[:], in0=vs[:].rearrange("p g t -> p (g t)"), in1=wsgn[:], op=ALU.mult
            )

        def write_abs():
            wflat = wr[:].rearrange("p g t -> p (g t)")
            wneg = cst.tile([P, TG * 4], F32, name="wneg")
            nc.vector.tensor_scalar(out=wneg[:], in0=wflat, scalar1=-1.0, scalar2=None, op0=ALU.mult)
            wabs = cst.tile([P, TG * 4], F32, name="wabs")
            nc.vector.tensor_tensor(out=wabs[:], in0=wflat, in1=wneg[:], op=ALU.max)
            wroot = cst.tile([P, TG * 4], F32, name="wroot")
            nc.gpsimd.tensor_tensor(out=wroot[:], in0=wabs[:], in1=quarter[:], op=ALU.pow)
            st["wroot"] = wroot

        def write_clip():
            wclip = cst.tile([P, TG * 4], F32, name="wclip")
            nc.vector.tensor_scalar(
                out=wclip[:], in0=st["wroot"][:], scalar1=1e-11, scalar2=None, op0=ALU.max
            )
            st["wclip"] = wclip

        def write_ln():
            wln = cst.tile([P, TG * 4], F32, name="wln")
            nc.scalar.activation(out=wln[:], in_=st["wclip"][:], func=ACTF.Ln)
            nc.scalar.activation(out=spare[:], in_=one[:], func=ACTF.Exp)
            st["wln"] = wln

        def write_bias():
            nc.vector.scalar_tensor_tensor(
                out=kbias[:], in0=st["wln"][:], scalar=4.0, in1=hn[:].rearrange("p g t -> p (g t)"),
                op0=ALU.mult, op1=ALU.subtract,
            )


        transposes(0)
        transposes(1)
        write_abs()
        sign_and_scale()
        copy_out(1)
        copy_out(0)
        quantize_rows(0)
        write_clip()
        quantize_rows(1)
        widen(3)
        widen(0)
        transposes(2)
        write_ln()
        key_product(1)
        permute_scales(1)
        write_bias()
        widen(1)
        permute_omega(1)
        transposes(3)
        key_exp(1, 0)
        permute_omega(0)
        key_exp(1, 1)
        copy_out(3)
        copy_out(2)
        widen(2)
        key_product(0)
        key_exp(0, 1)
        load_rows(2)
        transposes(5)
        key_exp(0, 0)
        transposes(6)
        quantize_rows(2)
        widen(7)
        key_product(2)
        transposes(7)
        values_interleave(0)
        widen(8)
        copy_out(5)
        key_exp(2, 1)
        values_quantize(0)
        transposes(4)
        transposes(8)
        key_exp(2, 0)
        copy_out(4)
        copy_out(8)
        key_product(3)
        quantize_rows(3)
        key_exp(3, 1)
        transposes(9)
        key_exp(3, 0)
        decay_split()
        copy_out(9)
        key_product(4)
        copy_out(7)
        transposes(11)
        key_exp(4, 0)
        quantize_rows(5)
        decay_eye()
        load_rows(3)
        key_exp(4, 1)
        key_product(5)
        copy_out(11)
        copy_out(6)
        key_exp(5, 1)
        decay_build()
        features_interleave(0, 0)
        key_exp(5, 0)
        transposes(10)
        quantize_rows(4)
        copy_out(10)
        widen(5)
        load_rows(4)
        key_product(7)
        key_exp(7, 0)
        transposes(13)
        decay_quantize()
        widen(6)
        key_exp(7, 1)
        widen(4)
        decay_place()
        widen(11)
        key_product(6)
        copy_out(13)
        key_exp(6, 0)
        key_exp(6, 1)
        quantize_rows(6)
        transposes(12)
        widen(10)
        copy_out(12)
        key_product(10)
        key_exp(10, 1)
        permute_scales(0)
        update_start(1, 0)
        features_quantize(0, 0)
        key_exp(10, 0)
        update_start(1, 1)
        key_product(8)
        update_start(2, 0)
        widen(9)
        values_interleave(1)
        load_rows(5)
        key_exp(8, 0)
        update_start(0, 1)
        key_exp(8, 1)
        update_start(2, 1)
        features_interleave(1, 0)
        values_quantize(1)
        load_rows(6)
        transposes(14)
        update_add(1, 1, 0)
        key_product(9)
        update_add(2, 1, 0)
        copy_out(14)
        update_add(0, 1, 0)
        key_exp(9, 0)
        transposes(15)
        features_quantize(1, 0)
        update_start(0, 0)
        key_exp(9, 1)
        update_add(0, 0, 0)
        key_product(11)
        update_add(1, 1, 1)
        copy_out(15)
        key_exp(11, 0)
        update_add(2, 1, 1)
        key_exp(11, 1)
        quantize_rows(7)
        transposes(16)
        update_add(0, 1, 1)
        update_add(1, 0, 0)
        copy_out(16)
        values_interleave(2)
        query_product(0)
        features_interleave(2, 0)
        query_exp(0, 1)
        values_quantize(2)
        update_add(0, 0, 1)
        features_quantize(2, 0)
        update_add(1, 0, 1)
        query_exp(0, 0)
        transposes(17)
        copy_out(17)
        update_add(2, 0, 0)
        load_rows(7)
        query_product(1)
        query_exp(1, 0)
        update_add(2, 0, 1)
        quantize_rows(8)
        update_add(2, 0, 2)
        query_scale(0)
        update_add(1, 0, 2)
        update_add(1, 1, 2)
        query_exp(1, 1)
        update_add(0, 1, 2)
        update_add(2, 1, 2)
        update_out(1, 0)
        query_quantize(0)
        update_out(1, 1)
        query_scale(1)
        update_add(0, 0, 2)
        update_out(2, 0)
        features_interleave(2, 1)
        query_product(2)
        transposes(18)
        read_product(0, 0)
        update_out(2, 1)
        read_product(0, 1)
        quantize_rows(9)
        query_exp(2, 1)
        query_exp(2, 0)
        read_square(0, 0)
        update_start(3, 0)
        query_quantize(1)
        features_quantize(2, 1)
        update_out(0, 0)
        update_add(3, 0, 0)
        read_square(0, 1)
        query_product(3)
        update_add(3, 0, 1)
        query_scale(2)
        update_add(3, 0, 2)
        update_out(0, 1)
        update_start(3, 1)
        copy_out(18)
        update_add(3, 1, 0)
        read_norm(0)
        read_product(1, 0)
        read_out(0, 0)
        query_quantize(2)
        read_out(0, 1)
        query_exp(3, 0)
        query_exp(3, 1)
        update_add(3, 1, 1)
        read_square(1, 0)
        read_product(1, 1)
        update_add(3, 1, 2)
        query_product(4)
        transposes(19)
        read_square(1, 1)
        query_scale(3)
        read_product(2, 0)
        read_norm(1)
        query_quantize(3)
        update_out(3, 0)
        read_out(1, 0)
        read_product(2, 1)
        read_out(1, 1)
        query_exp(4, 1)
        query_exp(4, 0)
        update_start(4, 0)
        read_square(2, 0)
        read_square(2, 1)
        update_add(4, 0, 0)
        update_add(4, 0, 1)
        query_scale(4)
        query_product(5)
        update_out(3, 1)
        update_add(4, 0, 2)
        copy_out(19)
        read_norm(2)
        update_start(4, 1)
        query_exp(5, 0)
        read_product(3, 0)
        query_exp(5, 1)
        quantize_rows(10)
        read_square(3, 0)
        read_product(3, 1)
        update_add(4, 1, 0)
        read_square(3, 1)
        query_quantize(4)
        read_norm(3)
        read_out(2, 0)
        read_out(2, 1)
        query_scale(5)
        query_quantize(5)
        update_add(4, 1, 1)
        update_add(4, 1, 2)
        query_product(6)
        read_product(4, 0)
        update_out(4, 0)
        update_start(5, 0)
        query_exp(6, 0)
        read_product(4, 1)
        update_add(5, 0, 0)
        read_out(3, 0)
        read_out(3, 1)
        update_add(5, 0, 1)
        query_exp(6, 1)
        read_square(4, 0)
        update_add(5, 0, 2)
        read_square(4, 1)
        update_out(4, 1)
        query_product(7)
        update_out(5, 0)
        read_product(5, 0)
        query_scale(6)
        read_product(5, 1)
        read_norm(4)
        read_square(5, 0)
        update_start(5, 1)
        read_square(5, 1)
        query_exp(7, 0)
        query_quantize(6)
        update_add(5, 1, 0)
        read_norm(5)
        read_out(4, 0)
        update_add(5, 1, 1)
        update_start(6, 0)
        update_add(6, 0, 0)
        read_out(4, 1)
        query_exp(7, 1)
        update_add(5, 1, 2)
        query_scale(7)
        read_product(6, 1)
        read_product(6, 0)
        read_out(5, 0)
        update_add(6, 0, 1)
        update_out(5, 1)
        query_quantize(7)
        read_square(6, 1)
        update_start(6, 1)
        update_add(6, 1, 0)
        update_add(6, 0, 2)
        read_square(6, 0)
        update_add(6, 1, 1)
        read_out(5, 1)
        update_out(6, 0)
        update_add(6, 1, 2)
        read_product(7, 1)
        update_out(6, 1)
        read_product(7, 0)
        update_start(7, 0)
        update_start(7, 1)
        update_add(7, 0, 0)
        update_add(7, 1, 0)
        read_square(7, 1)
        update_add(7, 0, 1)
        update_add(7, 0, 2)
        read_square(7, 0)
        read_norm(6)
        update_add(7, 1, 1)
        read_norm(7)
        read_out(6, 0)
        update_add(7, 1, 2)
        read_out(6, 1)
        update_out(7, 0)
        update_out(7, 1)
        read_out(7, 1)
        read_out(7, 0)
